import numpy as np
import ml_dtypes


def mxq(x, axis, fmt="e4m3"):
    dtype, down = {"e4m3": (ml_dtypes.float8_e4m3fn, 7), "e5m2": (ml_dtypes.float8_e5m2, 14)}[fmt]
    v = np.moveaxis(np.asarray(x, np.float32).astype(ml_dtypes.bfloat16).astype(np.float64), axis, -1)
    blocks = v.reshape(v.shape[:-1] + (-1, 32))
    amax = np.abs(blocks).max(-1, keepdims=True)
    byte = np.maximum(np.where(amax > 0, np.frexp(amax)[1] - 1 + 127, 0) - down, 1)
    scale = np.exp2(byte - 127.0)
    codes = (blocks / scale).astype(np.float32).astype(dtype).astype(np.float64)
    return np.moveaxis((codes * scale).reshape(v.shape), -1, axis)


WIDE = False


def mx_kscale(k):
    if not WIDE:
        return np.ones(k)
    levels = np.array([10, -10, 5, -5, 0])
    if k % 512:
        return np.exp2(np.random.permutation(np.resize(levels, k // 32))).repeat(32)
    a = np.empty((k // 512, 16))
    for p in range(k // 512):
        a[p, :8] = np.random.permutation(np.resize(levels, 8))
        for g in range(8):
            far = levels[np.abs(levels - a[p, g]) >= 10]
            a[p, g + 8] = far[np.random.randint(len(far))]
    return np.exp2(a.ravel()).repeat(32)


def f64(x):
    return np.asarray(x).astype(np.float64)


def striped(idx):
    return np.tile(idx.reshape(-1, 16).T, (8, 1)).astype(np.uint16)


def unstriped(offs):
    return offs[:16].T.reshape(-1).astype(np.int64)


E2M1 = np.array([0.0, 0.5, 1.0, 1.5, 2.0, 3.0, 4.0, 6.0, -0.0, -0.5, -1.0, -1.5, -2.0, -3.0, -4.0, -6.0])


def pack_weight(w, fmt):
    k, n = w.shape
    w = f64(np.asarray(w, np.float32).astype(ml_dtypes.bfloat16)).reshape(k // 32, 32, n)
    amax = np.abs(w).max(1)
    if fmt == "e4m3":
        byte = np.frexp(amax)[1] - 1 + 127 - 7
    else:
        mant, ex = np.frexp(amax / 6.0)
        byte = np.where(mant > 0.5, ex, ex - 1) + 127
    byte = np.clip(np.where(amax > 0, byte, 1), 1, 254)
    scaled = (w * np.exp2(127.0 - byte)[:, None, :]).reshape(k, n).astype(np.float32)
    by_word = np.ascontiguousarray(scaled.reshape(k // 512, 128, 4, n).transpose(0, 1, 3, 2))
    if fmt == "e4m3":
        words = by_word.astype(ml_dtypes.float8_e4m3fn).view(np.uint8)
    else:
        c = by_word.astype(ml_dtypes.float4_e2m1fn).view(np.uint8) & 0xF
        words = (c[..., 0::2] | (c[..., 1::2] << 4)).reshape(k // 512, 128, 2 * n)
    return np.ascontiguousarray(words), np.ascontiguousarray(byte.astype(np.uint8).reshape(k // 512, 16, n))


def unpack_weight(words, scales, fmt):
    g, _, n = scales.shape
    words = np.ascontiguousarray(words).reshape(g, 128, n, -1)
    if fmt == "e4m3":
        vals = words.view(ml_dtypes.float8_e4m3fn).astype(np.float64)
    else:
        nib = np.empty((g, 128, n, 4), np.uint8)
        nib[..., 0::2] = words & 0xF
        nib[..., 1::2] = words >> 4
        vals = E2M1[nib]
    vals = vals * np.repeat(np.exp2(scales.astype(np.float64) - 127.0), 8, axis=1)[..., None]
    return vals.transpose(0, 1, 3, 2).reshape(g * 512, n)


def gelu(v):
    return 0.5 * v * (1.0 + np.tanh(np.sqrt(2.0 / np.pi) * (v + 0.044715 * v**3)))


K, K2, T, T3, S, H, T2, P = 1536, 1024, 2048, 1024, 512, 1024, 2048, 512

def setup_inputs():
    n = np.random.standard_normal
    s, s2, u = mx_kscale(K)[:, None], mx_kscale(K2)[:, None], mx_kscale(H)[:, None]
    perm = np.random.permutation(T2)
    d = {}
    d["tab_words"], d["tab_scales"] = pack_weight(n((K, T)) * s, "e4m3")
    d["tab2_words"], d["tab2_scales"] = pack_weight(n((K2, T3)) * s2, "e4m3")
    d["offs"] = striped(np.random.permutation(T)[:S])
    d["offs2"] = striped(np.random.permutation(T3)[:S])
    d["offs3"] = striped(perm[:S])
    d["offs4"] = striped(perm[S:2 * S])
    d["offs5"] = striped(np.random.permutation(T2)[:P])
    d["w1"] = (1.5 * n((K, H)) / s / K**0.5).astype(np.float32)
    d["gain"] = (np.exp(0.4 * n(H)) * u[:, 0]).astype(np.float32)
    d["w2_words"], d["w2_scales"] = pack_weight(n((K2, H)) * u.T / s2 / K2**0.5, "e2m1")
    d["cm"] = np.exp(0.5 * n((H, S))).astype(np.float32)
    d["wg1"] = np.exp(0.3 * n((128, S))).astype(np.float32)
    d["wg2"] = np.exp(0.3 * n((128, S))).astype(np.float32)
    d["page0"] = (n((H, T2)) * u).astype(np.float32)
    d["level"] = ((0.5 * n(H) - 0.3) * u[:, 0]).astype(np.float32)
    d["w3"] = (n((H, H)) / u / H**0.5).astype(np.float32)
    d["own"] = (np.exp(0.3 * n(H)) / u[:, 0]).astype(np.float32)
    d["w4_words"], d["w4_scales"] = pack_weight(n((H, H)) / u / H**0.5, "e2m1")
    return d

def reference(tab_words, tab_scales, tab2_words, tab2_scales, offs, offs2, offs3, offs4, offs5, w1, gain,
              w2_words, w2_scales, cm, wg1, wg2, page0, level, w3, own, w4_words, w4_scales):
    v = unpack_weight(tab_words, tab_scales, "e4m3")[:, unstriped(offs)]
    v2 = unpack_weight(tab2_words, tab2_scales, "e4m3")[:, unstriped(offs2)]
    a = mxq(f64(w1), 0, "e4m3").T @ v
    h1 = f64(gain)[:, None] * (0.5 * a * (1.0 + np.tanh(0.7978845608028654 * (a + 0.044715 * a**3))))
    h2 = (unpack_weight(w2_words, w2_scales, "e2m1").T @ v2) * f64(cm)
    page = f64(page0).copy()
    page[:, unstriped(offs3)] = np.tile(f64(wg1), (H // 128, 1)) * h1
    page[:, unstriped(offs4)] = np.tile(f64(wg2), (H // 128, 1)) * h2
    x = np.maximum(page[:, unstriped(offs5)], f64(level)[:, None])
    xq = mxq(x, 0, "e4m3")
    y = mxq(f64(w3), 0, "e4m3").T @ xq
    best = np.maximum(y, f64(own)[:, None] * x)
    return best + (unpack_weight(w4_words, w4_scales, "e2m1").T @ xq)

@@ -1,0 +1,371 @@
+from contextlib import ExitStack
+
+import concourse.mybir as mybir
+from concourse.masks import make_identity
+
+K, K2, T, T3, S, H, T2 = 1536, 1024, 2048, 1024, 512, 1024, 2048
+FLOPS = 2 * S * H * (K + K2 + H + H)
+
+F32 = mybir.dt.float32
+BF16 = mybir.dt.bfloat16
+I32 = mybir.dt.int32
+U32 = mybir.dt.uint32
+U16 = mybir.dt.uint16
+U8 = mybir.dt.uint8
+FP8X4 = mybir.dt.float8_e4m3fn_x4
+FP4X4 = mybir.dt.float4_e2m1fn_x4
+ALU = mybir.AluOpType
+ACT = mybir.ActivationFunctionType
+
+P = 128
+PACK = 4
+KP = P * PACK
+
+
+def tile_list_dressage_board_scores_kernel(
+    tc, tab_words, tab_scales, tab2_words, tab2_scales, offs, offs2, offs3, offs4, offs5, w1, gain,
+    w2_words, w2_scales, cm, wg1, wg2, page0, level, w3, own, w4_words, w4_scales, out,
+):
+    nc = tc.nc
+    with ExitStack() as ctx:
+        lists = ctx.enter_context(tc.tile_pool(name="lists", bufs=1))
+        keep = ctx.enter_context(tc.tile_pool(name="keep", bufs=1))
+        psum = ctx.enter_context(tc.psum_pool(name="psum", bufs=1))
+
+        def sb(name, shape, dtype):
+            return keep.tile(shape, dtype, name=name, align_bytes=64)
+
+        idx1 = lists.tile([P, S // 16], U16, name="idx1")
+        idx2 = lists.tile([P, S // 16], U16, name="idx2")
+        idx3 = lists.tile([P, S // 16], U16, name="idx3")
+        idx4 = lists.tile([P, S // 16], U16, name="idx4")
+        idx5 = lists.tile([P, S // 16], U16, name="idx5")
+
+        bank = [psum.tile([P, S], F32, name="bank%d" % i) for i in range(8)]
+        page = [sb("page%d" % s, [P, T2], F32) for s in range(8)]
+        tabw = [sb("tabw%d" % a, [P, T], U32) for a in range(3)]
+        tab2w = [sb("tab2w%d" % a, [P, T3], U32) for a in range(2)]
+        tabs = sb("tabs", [P, T], U8)
+        tab2s = sb("tab2s", [P, 2 * T3], U8)
+        vw = [sb("vw%d" % a, [P, S], U32) for a in range(3)]
+        v2w = [sb("v2w%d" % a, [P, S], U32) for a in range(2)]
+        vs = sb("vs", [P, S], U8)
+        v2s = [sb("v2s%d" % a, [P, S], U8) for a in range(2)]
+        f4raw = [sb("f4raw%d" % b, [P, 2, 2 * KP], U8) for b in range(2)]
+        f4sraw = sb("f4sraw", [P, 2, H], U8)
+        f4w = [sb("f4w%d" % b, [P, 2, 2 * KP], U8) for b in range(2)]
+        f4s = [sb("f4s%d" % b, [P, 2, KP], U8) for b in range(2)]
+        stage = [sb("stage%d" % i, [P, PACK * KP], F32) for i in range(3)]
+        half = [sb("half%d" % i, [P, PACK * KP], BF16) for i in range(2)]
+        wq = [sb("wq%d" % i, [P, KP], U32) for i in range(7)]
+        wqs = [sb("wqs%d" % i, [P, KP], U8) for i in range(7)]
+        wgraw = [sb("wgraw%d" % i, [P, S], F32) for i in range(2)]
+        wg1d = sb("wg1d", [P, PACK * S], F32)
+        wgg0 = sb("wgg0", [P, PACK * S], F32)
+        hbuf = [sb("hbuf%d" % i, [P, S], F32) for i in range(4)]
+        xs = [sb("xs%d" % b, [P, PACK * S], F32) for b in range(2)]
+        xq = [sb("xq%d" % b, [P, S], U32) for b in range(2)]
+        xqs = [sb("xqs%d" % b, [P, S], U8) for b in range(2)]
+        gain_c = sb("gain_c", [P, 2, PACK], F32)
+        level_c = sb("level_c", [P, 2, PACK], F32)
+        own_c = sb("own_c", [P, 2, PACK], F32)
+        ident = sb("ident", [P, P], F32)
+        warm = sb("warm", [P, 1], F32)
+
+        def cols(tile, t):
+            return tile[:, t * S:(t + 1) * S]
+
+        def rows_of(mat, s):
+            b, t = divmod(s, PACK)
+            return mat[b * KP:(b + 1) * KP, :].rearrange("(p t) n -> p t n", t=PACK)[:, t, :]
+
+        def load_vec(dst, vec):
+            nc.sync.dma_start(out=dst[:], in_=vec.rearrange("(b p t) -> p b t", b=2, t=PACK))
+
+        def load_words(dst, words, a):
+            nc.sync.dma_start(out=dst[:].bitcast(I32), in_=words[a].rearrange("p n i -> p (n i)").bitcast(I32))
+
+        def load_planes_side_by_side(eng, dst, scales):
+            for q in range(4):
+                eng.dma_start(out=dst[32 * q:32 * q + 4, :, :].bitcast(I32),
+                              in_=scales[:, 4 * q:4 * q + 4, :].rearrange("a r n -> r a n").bitcast(I32))
+
+        def load_f4(words, b):
+            nc.sync.dma_start(out=f4raw[b][:].bitcast(I32),
+                              in_=words[:, :, 2 * KP * b:2 * KP * (b + 1)].rearrange("a p n -> p a n").bitcast(I32))
+
+        def deal_f4_words(b):
+            nc.vector.tensor_copy(out=f4w[b][:].bitcast(U16).rearrange("p a (t m) -> p a m t", t=PACK),
+                                  in_=f4raw[b][:].bitcast(U16).rearrange("p a (m t) -> p a m t", t=PACK))
+
+        def deal_f4_scales(b):
+            nc.vector.tensor_copy(out=f4s[b][:].rearrange("p a (t m) -> p a m t", t=PACK),
+                                  in_=f4sraw[:, :, KP * b:KP * (b + 1)].rearrange("p a (m t) -> p a m t", t=PACK))
+
+        def f4_pass(acc, s, a, rhs, rhs_scale, start, stop):
+            b, t = divmod(s, PACK)
+            nc.tensor.matmul_mx(out=acc[:], lhsT=f4w[b][:, a, 2 * P * t:2 * P * (t + 1)].bitcast(FP4X4),
+                                lhsT_scale=f4s[b][:, a, P * t:P * (t + 1)],
+                                rhs=rhs.bitcast(FP8X4), rhs_scale=rhs_scale, start=start, stop=stop)
+
+        def f8_pass(acc, slot, t, rhs, rhs_scale, start, stop):
+            nc.tensor.matmul_mx(out=acc[:], lhsT=wq[slot][:, P * t:P * (t + 1)].bitcast(FP8X4),
+                                lhsT_scale=wqs[slot][:, P * t:P * (t + 1)],
+                                rhs=rhs.bitcast(FP8X4), rhs_scale=rhs_scale, start=start, stop=stop)
+
+        def spread_wg(raw, rep, banks):
+            for c in range(4):
+                nc.tensor.transpose(banks[3][:, P * c:P * (c + 1)], raw[:, P * c:P * (c + 1)], ident[:])
+            nc.scalar.copy(
+                out=rep[:].rearrange("p (c t q m) -> p c q m t", c=4, t=PACK, q=4),
+                in_=banks[3][:].rearrange("p (c m t) -> p c m t", c=4, t=PACK).unsqueeze(2).to_broadcast([P, 4, 4, 32, PACK]))
+            for t in range(PACK):
+                for c in range(4):
+                    nc.tensor.transpose(banks[t][:, P * c:P * (c + 1)], rep[:, S * c + P * t:S * c + P * (t + 1)], ident[:])
+
+        def load_w(w, a, b, raw):
+            nc.sync.dma_start(out=raw[:].rearrange("p (i n) -> p i n", i=PACK),
+                              in_=w[KP * a:KP * (a + 1), KP * b:KP * (b + 1)].rearrange("(p i) n -> p i n", i=PACK))
+
+        def cast_w(raw, grouped):
+            nc.scalar.copy(out=grouped.rearrange("p (t m i) -> p m i t", t=PACK, i=PACK),
+                           in_=raw[:].rearrange("p (i m t) -> p m i t", i=PACK, t=PACK))
+
+        def quant(codes, scales, grouped):
+            nc.vector.quantize_mx(out=codes[:].bitcast(FP8X4), scales=scales[:], in_=grouped)
+
+        def load_cm(s):
+            nc.sync.dma_start(out=cols(xs[0], s % PACK), in_=rows_of(cm, s))
+
+        def load_page(s):
+            nc.sync.dma_start(out=page[s][:], in_=rows_of(page0, s))
+
+        def h2_product(s):
+            for a in range(2):
+                f4_pass(bank[s % 4], s, a, v2w[a][:], v2s[a][:], a == 0, a == 1)
+            nc.vector.tensor_tensor(out=hbuf[s % 4][:], in0=bank[s % 4][:], in1=cols(xs[0], s % PACK), op=ALU.mult)
+
+        def h2_put(s):
+            nc.vector.tensor_tensor(out=page[s][:].indirect(idx4[:]), in0=hbuf[s % 4][:],
+                                    in1=cols(xs[1], s % PACK), op=ALU.mult)
+
+        def gather_tab(a):
+            nc.vector.tensor_copy(out=vw[a][:], in_=tabw[a][:].indirect(idx1[:]))
+
+        def h1_pass(s, a, start, stop):
+            b, t = divmod(s, PACK)
+            f8_pass(bank[(4 + s) % 8], 3 * b + a, t, vw[a][:], vs[4 * a:P, :], start, stop)
+
+        def gelu(s):
+            nc.scalar.activation(out=hbuf[s % 4][:], in_=bank[(4 + s) % 8][:], func=ACT.Gelu_apprx_tanh)
+
+        def h1_put(s, wgg):
+            nc.vector.tensor_tensor(out=page[s][:].indirect(idx3[:]), in0=hbuf[s % 4][:],
+                                    in1=cols(wgg, s % PACK), op=ALU.mult)
+
+        def fetch(s):
+            b, t = divmod(s, PACK)
+            nc.vector.tensor_copy(out=cols(xs[b], t), in_=page[s][:].indirect(idx5[:]))
+
+        def floor(s):
+            b, t = divmod(s, PACK)
+            nc.vector.tensor_scalar(out=cols(xs[b], t), in0=cols(xs[b], t), scalar1=level_c[:, b, t:t + 1],
+                                    scalar2=None, op0=ALU.max)
+
+        def cast_x(b, grouped):
+            nc.scalar.copy(out=grouped.rearrange("p (c i t) -> p c t i", i=4, t=PACK),
+                           in_=xs[b][:].rearrange("p (t c i) -> p c t i", t=PACK, i=4))
+
+        def as_bf16(tile, k):
+            return tile[:, 1024 * k:1024 * (k + 1)].bitcast(BF16)
+
+        nc.vector.memset(tab2s[:].bitcast(I32), 0)
+        nc.vector.memset(f4sraw[:].rearrange("p a n -> p (a n)").bitcast(I32), 0)
+        make_identity(nc, ident[:])
+        nc.vector.memset(warm[:], 0.0)
+        nc.vector.memset(tabs[:].bitcast(I32), 0)
+        nc.scalar.activation(out=warm[:], in_=warm[:], func=ACT.Gelu_apprx_tanh)
+        load_words(tab2w[0], tab2_words, 0)
+        load_planes_side_by_side(nc.sync, tab2s[:].rearrange("p (a n) -> p a n", a=2), tab2_scales)
+        nc.sync.dma_start(idx2[:], offs2)
+        load_f4(w2_words, 0)
+        nc.sync.dma_start(out=wgraw[1][:], in_=wg2)
+        load_planes_side_by_side(nc.sync, f4sraw, w2_scales)
+        load_words(tab2w[1], tab2_words, 1)
+        nc.sync.dma_start(idx4[:], offs4)
+        load_cm(0)
+        load_page(0)
+
+        spread_wg(wgraw[1], stage[0], bank[4:8])
+        for t in range(PACK):
+            nc.scalar.copy(out=cols(xs[1], t), in_=bank[4 + t][:])
+
+        for a in range(2):
+            nc.vector.tensor_copy(out=v2s[a][:], in_=tab2s[:, T3 * a:T3 * (a + 1)].indirect(idx2[:]))
+        nc.vector.tensor_copy(out=v2w[0][:], in_=tab2w[0][:].indirect(idx2[:]))
+        deal_f4_words(0)
+        deal_f4_scales(0)
+        nc.vector.tensor_copy(out=v2w[1][:], in_=tab2w[1][:].indirect(idx2[:]))
+
+        h2_product(0)
+        load_cm(1)
+        load_cm(2)
+        load_page(1)
+        h2_put(0)
+        h2_product(1)
+        load_f4(w2_words, 1)
+        load_cm(3)
+        load_page(2)
+        h2_product(2)
+        h2_put(1)
+        deal_f4_words(1)
+        deal_f4_scales(1)
+        nc.sync.dma_start(out=wgraw[0][:], in_=wg1)
+        load_vec(gain_c, gain)
+        nc.sync.dma_start(idx1[:], offs)
+        for q in range(4):
+            nc.sync.dma_start(out=tabs[32 * q:32 * q + 12, :].bitcast(I32),
+                              in_=tab_scales[:, 4 * q:4 * q + 4, :].bitcast(I32))
+        load_words(tabw[0], tab_words, 0)
+        h2_product(3)
+        h2_put(2)
+        spread_wg(wgraw[0], stage[1], bank[4:8])
+        for t in range(PACK):
+            nc.scalar.copy(out=cols(wg1d, t), in_=bank[4 + t][:])
+            nc.scalar.activation(out=cols(wgg0, t), in_=bank[4 + t][:], func=ACT.Copy, scale=gain_c[:, 0, t:t + 1])
+        nc.vector.tensor_copy(out=vs[:], in_=tabs[:].indirect(idx1[:]))
+        gather_tab(0)
+        load_cm(4)
+        load_page(3)
+        load_words(tabw[1], tab_words, 1)
+        h2_product(4)
+        h2_put(3)
+        gather_tab(1)
+        load_cm(5)
+        load_page(4)
+        load_words(tabw[2], tab_words, 2)
+        h2_product(5)
+        h2_put(4)
+        gather_tab(2)
+
+        def w1_chunk(a, b, raw, grouped):
+            cast_w(raw, grouped)
+            quant(wq[3 * b + a], wqs[3 * b + a], grouped)
+
+        load_w(w1, 0, 0, stage[2])
+        load_cm(6)
+        load_page(5)
+        load_w(w1, 1, 0, stage[0])
+        h2_product(6)
+        h2_put(5)
+        w1_chunk(0, 0, stage[2], half[0][:])
+        for s in range(4):
+            h1_pass(s, 0, True, False)
+        load_cm(7)
+        load_page(6)
+        load_w(w1, 2, 0, stage[1])
+        h2_product(7)
+        h2_put(6)
+        w1_chunk(1, 0, stage[0], half[1][:])
+        for s in range(4):
+            h1_pass(s, 1, False, False)
+        nc.sync.dma_start(idx3[:], offs3)
+        load_page(7)
+        nc.sync.dma_start(idx5[:], offs5)
+        load_vec(level_c, level)
+        w1_chunk(2, 0, stage[1], half[0][:])
+        h2_put(7)
+        for s in range(4):
+            h1_pass(s, 2, False, True)
+            gelu(s)
+
+        load_w(w1, 0, 1, stage[2])
+        load_w(w1, 1, 1, stage[0])
+        load_w(w1, 2, 1, stage[1])
+        h1_put(0, wgg0)
+        h1_put(1, wgg0)
+        fetch(0)
+        fetch(1)
+        floor(0)
+        h1_put(2, wgg0)
+        floor(1)
+        h1_put(3, wgg0)
+        w1_chunk(0, 1, stage[2], half[1][:])
+        w1_chunk(1, 1, stage[0], half[0][:])
+        w1_chunk(2, 1, stage[1], as_bf16(xs[0], 1))
+        wgg1 = stage[1]
+        for t in range(PACK):
+            nc.scalar.activation(out=cols(wgg1, t), in_=cols(wg1d, t), func=ACT.Copy, scale=gain_c[:, 1, t:t + 1])
+        fetch(2)
+        fetch(3)
+        floor(2)
+        floor(3)
+        for s in range(4, 8):
+            for n, a in enumerate((2, 0, 1)):
+                h1_pass(s, a, n == 0, n == 2)
+            gelu(s)
+
+        load_f4(w4_words, 0)
+        load_f4(w4_words, 1)
+        load_planes_side_by_side(nc.sync, f4sraw, w4_scales)
+        load_vec(own_c, own)
+        for b in range(2):
+            deal_f4_words(b)
+            deal_f4_scales(b)
+        cast_x(0, half[1][:])
+        quant(xq[0], xqs[0], half[1][:])
+        for s in range(4, 8):
+            h1_put(s, wgg1)
+
+        w3_slot = {(0, 0): 6, (1, 0): 0, (0, 1): 1, (1, 1): 2}
+        w3_raw = {(0, 0): stage[2], (1, 0): stage[0], (0, 1): stage[2], (1, 1): stage[0]}
+        w3_half = {(0, 0): as_bf16(xs[1], 0), (1, 0): as_bf16(xs[1], 1), (0, 1): half[0][:], (1, 1): half[1][:]}
+
+        def w3_chunk(a, b):
+            load_w(w3, a, b, w3_raw[a, b])
+            cast_w(w3_raw[a, b], w3_half[a, b])
+            quant(wq[w3_slot[a, b]], wqs[w3_slot[a, b]], w3_half[a, b])
+
+        def y_pass(s, a):
+            b, t = divmod(s, PACK)
+            f8_pass(bank[4 + t], w3_slot[a, b], t, xq[a][:], xqs[a][:], a == 0, a == 1)
+            f4_pass(bank[t], s, a, xq[a][:], xqs[a][:], a == 0, a == 1)
+
+        w3_chunk(0, 0)
+        fetch(4)
+        fetch(5)
+        for s in range(4):
+            y_pass(s, 0)
+        w3_chunk(1, 0)
+        floor(4)
+        floor(5)
+        fetch(6)
+        fetch(7)
+        floor(6)
+        floor(7)
+        w3_chunk(0, 1)
+        w3_chunk(1, 1)
+        x1_half = as_bf16(stage[0], 0)
+        cast_x(1, x1_half)
+        quant(xq[1], xqs[1], x1_half)
+
+        def meet(s):
+            b, t = divmod(s, PACK)
+            nc.vector.scalar_tensor_tensor(out=cols(xs[b], t), in0=cols(xs[b], t), scalar=own_c[:, b, t:t + 1],
+                                           in1=bank[4 + t][:], op0=ALU.mult, op1=ALU.max)
+
+        def finish(s):
+            b, t = divmod(s, PACK)
+            nc.vector.tensor_tensor(out=cols(xs[b], t), in0=bank[t][:], in1=cols(xs[b], t), op=ALU.add)
+            nc.sync.dma_start(out=rows_of(out, s), in_=cols(xs[b], t))
+
+        for s in range(4):
+            y_pass(s, 1)
+        meet(0)
+        for s in range(8):
+            if s + 1 < 8:
+                if s + 1 >= 4:
+                    y_pass(s + 1, 0)
+                    y_pass(s + 1, 1)
+                meet(s + 1)
+            finish(s)

@@ -20,6 +20,9 @@ ACT = mybir.ActivationFunctionType
 P = 128
 PACK = 4
 KP = P * PACK
+GW = 256
+SPLIT = 144
+POOL_ADDS = 3
 
 
 def tile_list_dressage_board_scores_kernel(
@@ -51,36 +54,36 @@ def tile_list_dressage_board_scores_kernel(
         v2w = [sb("v2w%d" % a, [P, S], U32) for a in range(2)]
         vs = sb("vs", [P, S], U8)
         v2s = [sb("v2s%d" % a, [P, S], U8) for a in range(2)]
-        f4raw = [sb("f4raw%d" % b, [P, 2, 2 * KP], U8) for b in range(2)]
-        f4sraw = sb("f4sraw", [P, 2, H], U8)
         f4w = [sb("f4w%d" % b, [P, 2, 2 * KP], U8) for b in range(2)]
-        f4s = [sb("f4s%d" % b, [P, 2, KP], U8) for b in range(2)]
+        f4s = sb("f4s", [P, 2, H], U8)
         stage = [sb("stage%d" % i, [P, PACK * KP], F32) for i in range(3)]
-        half = [sb("half%d" % i, [P, PACK * KP], BF16) for i in range(2)]
-        wq = [sb("wq%d" % i, [P, KP], U32) for i in range(7)]
-        wqs = [sb("wqs%d" % i, [P, KP], U8) for i in range(7)]
-        wgraw = [sb("wgraw%d" % i, [P, S], F32) for i in range(2)]
-        wg1d = sb("wg1d", [P, PACK * S], F32)
-        wgg0 = sb("wgg0", [P, PACK * S], F32)
-        hbuf = [sb("hbuf%d" % i, [P, S], F32) for i in range(4)]
-        xs = [sb("xs%d" % b, [P, PACK * S], F32) for b in range(2)]
+        w1half = [sb("w1half%d" % i, [P, PACK * GW], BF16) for i in range(5)]
+        w3half = [sb("w3half%d" % i, [P, PACK * KP], F32) for i in range(2)]
+        w1q = [sb("w1q%d" % i, [P, 3 * GW], U32) for i in range(2)]
+        w1qs = [sb("w1qs%d" % i, [P, 3 * KP], U8) for i in range(2)]
+        w3q = [sb("w3q%d" % i, [P, KP], U32) for i in range(3)]
+        wg1s = sb("wg1s", [P, S], F32)
+        wg2s = sb("wg2s", [P, S], F32)
+        hbuf = [sb("hbuf%d" % i, [P, S], F32) for i in range(3)]
+        hbuf.append(keep.tile([P, S], F32, name="hbuf3", tag="h_last", align_bytes=64))
+        xn = [sb("xn%d" % b, [P, PACK * S], F32) for b in range(2)]
+        xd = [stage[2], sb("xd1", [P, PACK * S], F32)]
         xq = [sb("xq%d" % b, [P, S], U32) for b in range(2)]
-        xqs = [sb("xqs%d" % b, [P, S], U8) for b in range(2)]
-        gain_c = sb("gain_c", [P, 2, PACK], F32)
-        level_c = sb("level_c", [P, 2, PACK], F32)
-        own_c = sb("own_c", [P, 2, PACK], F32)
+        xqs1 = sb("xqs1", [P, S], U8)
         ident = sb("ident", [P, P], F32)
+        vec_rows = sb("vec_rows", [P, P], F32)
+        vec_cols = sb("vec_cols", [P, 24], F32)
+        gain_c, level_c, own_c = vec_cols[:, 0:8], vec_cols[:, 8:16], vec_cols[:, 16:24]
         warm = sb("warm", [P, 1], F32)
 
         def cols(tile, t):
             return tile[:, t * S:(t + 1) * S]
 
-        def rows_of(mat, s):
-            b, t = divmod(s, PACK)
-            return mat[b * KP:(b + 1) * KP, :].rearrange("(p t) n -> p t n", t=PACK)[:, t, :]
+        def slot(pair, s):
+            return cols(pair[s // PACK], s % PACK)
 
-        def load_vec(dst, vec):
-            nc.sync.dma_start(out=dst[:], in_=vec.rearrange("(b p t) -> p b t", b=2, t=PACK))
+        def rows_of(mat, s):
+            return mat[P * s:P * (s + 1), :]
 
         def load_words(dst, words, a):
             nc.sync.dma_start(out=dst[:].bitcast(I32), in_=words[a].rearrange("p n i -> p (n i)").bitcast(I32))
@@ -90,282 +93,274 @@ def tile_list_dressage_board_scores_kernel(
                 eng.dma_start(out=dst[32 * q:32 * q + 4, :, :].bitcast(I32),
                               in_=scales[:, 4 * q:4 * q + 4, :].rearrange("a r n -> r a n").bitcast(I32))
 
+        def load_planes_packed(dst, scales, passes):
+            for q in range(4):
+                nc.sync.dma_start(out=dst[32 * q:32 * q + 4 * passes, :].bitcast(I32),
+                                  in_=scales[:, 4 * q:4 * q + 4, :].bitcast(I32))
+
         def load_f4(words, b):
-            nc.sync.dma_start(out=f4raw[b][:].bitcast(I32),
+            nc.sync.dma_start(out=f4w[b][:].bitcast(I32),
                               in_=words[:, :, 2 * KP * b:2 * KP * (b + 1)].rearrange("a p n -> p a n").bitcast(I32))
 
-        def deal_f4_words(b):
-            nc.vector.tensor_copy(out=f4w[b][:].bitcast(U16).rearrange("p a (t m) -> p a m t", t=PACK),
-                                  in_=f4raw[b][:].bitcast(U16).rearrange("p a (m t) -> p a m t", t=PACK))
-
-        def deal_f4_scales(b):
-            nc.vector.tensor_copy(out=f4s[b][:].rearrange("p a (t m) -> p a m t", t=PACK),
-                                  in_=f4sraw[:, :, KP * b:KP * (b + 1)].rearrange("p a (m t) -> p a m t", t=PACK))
-
-        def f4_pass(acc, s, a, rhs, rhs_scale, start, stop):
+        def f4_pass(acc, s, a, rhs, rhs_scale):
             b, t = divmod(s, PACK)
             nc.tensor.matmul_mx(out=acc[:], lhsT=f4w[b][:, a, 2 * P * t:2 * P * (t + 1)].bitcast(FP4X4),
-                                lhsT_scale=f4s[b][:, a, P * t:P * (t + 1)],
-                                rhs=rhs.bitcast(FP8X4), rhs_scale=rhs_scale, start=start, stop=stop)
+                                lhsT_scale=f4s[:, a, P * s:P * (s + 1)],
+                                rhs=rhs.bitcast(FP8X4), rhs_scale=rhs_scale, start=a == 0, stop=a == 1)
 
-        def f8_pass(acc, slot, t, rhs, rhs_scale, start, stop):
-            nc.tensor.matmul_mx(out=acc[:], lhsT=wq[slot][:, P * t:P * (t + 1)].bitcast(FP8X4),
-                                lhsT_scale=wqs[slot][:, P * t:P * (t + 1)],
-                                rhs=rhs.bitcast(FP8X4), rhs_scale=rhs_scale, start=start, stop=stop)
+        def load_w(w, a, lo, width, raw):
+            nc.sync.dma_start(out=raw.rearrange("p (i n) -> p i n", i=PACK),
+                              in_=w[KP * a:KP * (a + 1), lo:lo + width].rearrange("(p i) n -> p i n", i=PACK))
 
-        def spread_wg(raw, rep, banks):
-            for c in range(4):
-                nc.tensor.transpose(banks[3][:, P * c:P * (c + 1)], raw[:, P * c:P * (c + 1)], ident[:])
-            nc.scalar.copy(
-                out=rep[:].rearrange("p (c t q m) -> p c q m t", c=4, t=PACK, q=4),
-                in_=banks[3][:].rearrange("p (c m t) -> p c m t", c=4, t=PACK).unsqueeze(2).to_broadcast([P, 4, 4, 32, PACK]))
-            for t in range(PACK):
-                for c in range(4):
-                    nc.tensor.transpose(banks[t][:, P * c:P * (c + 1)], rep[:, S * c + P * t:S * c + P * (t + 1)], ident[:])
-
-        def load_w(w, a, b, raw):
-            nc.sync.dma_start(out=raw[:].rearrange("p (i n) -> p i n", i=PACK),
-                              in_=w[KP * a:KP * (a + 1), KP * b:KP * (b + 1)].rearrange("(p i) n -> p i n", i=PACK))
-
-        def cast_w(raw, grouped):
-            nc.scalar.copy(out=grouped.rearrange("p (t m i) -> p m i t", t=PACK, i=PACK),
-                           in_=raw[:].rearrange("p (i m t) -> p m i t", i=PACK, t=PACK))
+        def weave(copy, src, grouped, lo, hi):
+            copy(out=grouped.rearrange("p (c i t) -> p c t i", i=4, t=PACK)[:, lo // 4:hi // 4, :, :],
+                 in_=src.rearrange("p (t c i) -> p c t i", t=PACK, i=4)[:, lo // 4:hi // 4, :, :])
 
         def quant(codes, scales, grouped):
-            nc.vector.quantize_mx(out=codes[:].bitcast(FP8X4), scales=scales[:], in_=grouped)
+            nc.vector.quantize_mx(out=codes.bitcast(FP8X4), scales=scales, in_=grouped)
+
+        def as_bf16(tile, lo, words):
+            return tile[:, lo:lo + words].bitcast(BF16)
 
         def load_cm(s):
-            nc.sync.dma_start(out=cols(xs[0], s % PACK), in_=rows_of(cm, s))
+            nc.sync.dma_start(out=cols(xn[1], s % PACK), in_=rows_of(cm, s))
 
-        def load_page(s):
+        def load_board(s):
+            if s + 1 < 8:
+                load_cm(s + 1)
             nc.sync.dma_start(out=page[s][:], in_=rows_of(page0, s))
 
         def h2_product(s):
             for a in range(2):
-                f4_pass(bank[s % 4], s, a, v2w[a][:], v2s[a][:], a == 0, a == 1)
-            nc.vector.tensor_tensor(out=hbuf[s % 4][:], in0=bank[s % 4][:], in1=cols(xs[0], s % PACK), op=ALU.mult)
+                f4_pass(bank[s % 4], s, a, v2w[a][:], v2s[a][:])
+            nc.vector.tensor_tensor(out=hbuf[s % 2][:], in0=bank[s % 4][:], in1=cols(xn[1], s % PACK), op=ALU.mult)
 
         def h2_put(s):
-            nc.vector.tensor_tensor(out=page[s][:].indirect(idx4[:]), in0=hbuf[s % 4][:],
-                                    in1=cols(xs[1], s % PACK), op=ALU.mult)
+            if s + 1 < 5:
+                h2_product(s + 1)
+            nc.vector.tensor_tensor(out=page[s][:].indirect(idx4[:]), in0=hbuf[s % 2][:], in1=wg2s[:], op=ALU.mult)
 
         def gather_tab(a):
             nc.vector.tensor_copy(out=vw[a][:], in_=tabw[a][:].indirect(idx1[:]))
 
+        wgg = [w3half[1], sb("wgg1", [P, PACK * S], F32)]
+
+        def w1_codes(g, a):
+            return w1q[g % 2][:, GW * a:GW * (a + 1)], w1qs[g % 2][:, KP * a:KP * a + GW]
+
+        def w1_chunk(g, a, unit, grouped):
+            raw = stage[unit // 2][:, 1024 * (unit % 2):1024 * (unit % 2 + 1)]
+            load_w(w1, a, GW * g, GW, raw)
+            weave(nc.scalar.copy, raw, grouped, 0, GW)
+            codes, scales = w1_codes(g, a)
+            quant(codes, scales, grouped)
+
         def h1_pass(s, a, start, stop):
-            b, t = divmod(s, PACK)
-            f8_pass(bank[(4 + s) % 8], 3 * b + a, t, vw[a][:], vs[4 * a:P, :], start, stop)
+            codes, scales = w1_codes(s // 2, a)
+            m = slice(P * (s % 2), P * (s % 2 + 1))
+            nc.tensor.matmul_mx(out=bank[4 + s % 4][:], lhsT=codes[:, m].bitcast(FP8X4), lhsT_scale=scales[:, m],
+                                rhs=vw[a][:].bitcast(FP8X4), rhs_scale=vs[4 * a:P, :], start=start, stop=stop)
 
         def gelu(s):
-            nc.scalar.activation(out=hbuf[s % 4][:], in_=bank[(4 + s) % 8][:], func=ACT.Gelu_apprx_tanh)
+            nc.scalar.activation(out=hbuf[2 + s % 2][:], in_=bank[4 + s % 4][:], func=ACT.Gelu_apprx_tanh)
 
-        def h1_put(s, wgg):
-            nc.vector.tensor_tensor(out=page[s][:].indirect(idx3[:]), in0=hbuf[s % 4][:],
-                                    in1=cols(wgg, s % PACK), op=ALU.mult)
+        def h1_group(g):
+            for s in (2 * g, 2 * g + 1):
+                for n, a in enumerate((2, 0, 1)):
+                    h1_pass(s, a, n == 0, n == 2)
+                gelu(s)
+
+        def h1_put(s):
+            nc.vector.tensor_tensor(out=page[s][:].indirect(idx3[:]), in0=hbuf[2 + s % 2][:],
+                                    in1=slot(wgg, s), op=ALU.mult)
 
         def fetch(s):
-            b, t = divmod(s, PACK)
-            nc.vector.tensor_copy(out=cols(xs[b], t), in_=page[s][:].indirect(idx5[:]))
+            nc.vector.tensor_copy(out=slot(xn, s), in_=page[s][:].indirect(idx5[:]))
 
         def floor(s):
-            b, t = divmod(s, PACK)
-            nc.vector.tensor_scalar(out=cols(xs[b], t), in0=cols(xs[b], t), scalar1=level_c[:, b, t:t + 1],
+            nc.vector.tensor_scalar(out=slot(xn, s), in0=slot(xn, s), scalar1=level_c[:, s:s + 1],
                                     scalar2=None, op0=ALU.max)
 
-        def cast_x(b, grouped):
-            nc.scalar.copy(out=grouped.rearrange("p (c i t) -> p c t i", i=4, t=PACK),
-                           in_=xs[b][:].rearrange("p (t c i) -> p c t i", t=PACK, i=4))
+        def deal(eng, s):
+            b, q = divmod(s, PACK)
+            for t in range(PACK):
+                eng.dma_start(out=cols(xd[b], t)[32 * q:32 * (q + 1), :], in_=slot(xn, s)[t:P:PACK, :])
 
-        def as_bf16(tile, k):
-            return tile[:, 1024 * k:1024 * (k + 1)].bitcast(BF16)
+        def read_pair(s):
+            fetch(s)
+            fetch(s + 1)
+            floor(s)
+            floor(s + 1)
+
+        w3_codes = {(0, 0): w3q[0][:], (1, 0): w3q[1][:], (0, 1): w3q[2][:], (1, 1): w1q[1][:, 0:KP]}
+        w3_half = {(0, 0): as_bf16(w3half[0], 0, 1024), (1, 0): as_bf16(w3half[0], 1024, 1024),
+                   (0, 1): as_bf16(w3half[1], 0, 1024), (1, 1): as_bf16(w3half[1], 1024, 1024)}
+
+        def w3_round(a, b, raw):
+            load_w(w3, a, KP * b, KP, raw[:])
+            weave(nc.scalar.copy, raw[:], w3_half[a, b], 0, KP)
+
+        def y_pass(c, a):
+            b, t = divmod(c, PACK)
+            m = slice(P * t, P * (t + 1))
+            nc.tensor.matmul_mx(out=bank[4 + t][:], lhsT=w3_codes[a, b][:, m].bitcast(FP8X4),
+                                lhsT_scale=w3_scales[a, b][:, m],
+                                rhs=xq[a][:].bitcast(FP8X4), rhs_scale=xqs[a], start=a == 0, stop=a == 1)
+
+        def y4_pass(c, a):
+            f4_pass(bank[c % 4], c, a, xq[a][:], xqs[a])
 
         nc.vector.memset(tab2s[:].bitcast(I32), 0)
-        nc.vector.memset(f4sraw[:].rearrange("p a n -> p (a n)").bitcast(I32), 0)
-        make_identity(nc, ident[:])
+        nc.vector.memset(f4s[:].rearrange("p a n -> p (a n)").bitcast(I32), 0)
         nc.vector.memset(warm[:], 0.0)
+        make_identity(nc, ident[:])
+        nc.gpsimd.memset(vec_rows[:], 0.0)
         nc.vector.memset(tabs[:].bitcast(I32), 0)
         nc.scalar.activation(out=warm[:], in_=warm[:], func=ACT.Gelu_apprx_tanh)
         load_words(tab2w[0], tab2_words, 0)
         load_planes_side_by_side(nc.sync, tab2s[:].rearrange("p (a n) -> p a n", a=2), tab2_scales)
         nc.sync.dma_start(idx2[:], offs2)
-        load_f4(w2_words, 0)
-        nc.sync.dma_start(out=wgraw[1][:], in_=wg2)
-        load_planes_side_by_side(nc.sync, f4sraw, w2_scales)
         load_words(tab2w[1], tab2_words, 1)
-        nc.sync.dma_start(idx4[:], offs4)
+        load_f4(w2_words, 0)
+        load_planes_side_by_side(nc.sync, f4s, w2_scales)
+        nc.sync.dma_start(out=page[0][:], in_=rows_of(page0, 0))
         load_cm(0)
-        load_page(0)
-
-        spread_wg(wgraw[1], stage[0], bank[4:8])
-        for t in range(PACK):
-            nc.scalar.copy(out=cols(xs[1], t), in_=bank[4 + t][:])
+        nc.sync.dma_start(out=wg2s[:], in_=wg2)
+        nc.sync.dma_start(idx4[:], offs4)
+        load_cm(1)
 
         for a in range(2):
+            nc.vector.tensor_copy(out=v2w[a][:], in_=tab2w[a][:].indirect(idx2[:]))
             nc.vector.tensor_copy(out=v2s[a][:], in_=tab2s[:, T3 * a:T3 * (a + 1)].indirect(idx2[:]))
-        nc.vector.tensor_copy(out=v2w[0][:], in_=tab2w[0][:].indirect(idx2[:]))
-        deal_f4_words(0)
-        deal_f4_scales(0)
-        nc.vector.tensor_copy(out=v2w[1][:], in_=tab2w[1][:].indirect(idx2[:]))
 
         h2_product(0)
-        load_cm(1)
-        load_cm(2)
-        load_page(1)
         h2_put(0)
-        h2_product(1)
-        load_f4(w2_words, 1)
-        load_cm(3)
-        load_page(2)
-        h2_product(2)
+        load_board(1)
         h2_put(1)
-        deal_f4_words(1)
-        deal_f4_scales(1)
-        nc.sync.dma_start(out=wgraw[0][:], in_=wg1)
-        load_vec(gain_c, gain)
-        nc.sync.dma_start(idx1[:], offs)
-        for q in range(4):
-            nc.sync.dma_start(out=tabs[32 * q:32 * q + 12, :].bitcast(I32),
-                              in_=tab_scales[:, 4 * q:4 * q + 4, :].bitcast(I32))
-        load_words(tabw[0], tab_words, 0)
-        h2_product(3)
+        load_board(2)
         h2_put(2)
-        spread_wg(wgraw[0], stage[1], bank[4:8])
-        for t in range(PACK):
-            nc.scalar.copy(out=cols(wg1d, t), in_=bank[4 + t][:])
-            nc.scalar.activation(out=cols(wgg0, t), in_=bank[4 + t][:], func=ACT.Copy, scale=gain_c[:, 0, t:t + 1])
+        nc.sync.dma_start(idx1[:], offs)
+        load_planes_packed(tabs, tab_scales, 3)
+        load_words(tabw[0], tab_words, 0)
         nc.vector.tensor_copy(out=vs[:], in_=tabs[:].indirect(idx1[:]))
         gather_tab(0)
-        load_cm(4)
-        load_page(3)
-        load_words(tabw[1], tab_words, 1)
-        h2_product(4)
+        load_f4(w2_words, 1)
+        load_board(3)
         h2_put(3)
+        nc.sync.dma_start(out=wg1s[:], in_=wg1)
+        for n, vec in enumerate((gain, level, own)):
+            nc.sync.dma_start(out=vec_rows[8 * n:8 * (n + 1), :], in_=vec.rearrange("(s p) -> s p", p=P))
+        nc.tensor.transpose(bank[7][:, 0:P], vec_rows[:], ident[:])
+        nc.scalar.copy(out=vec_cols[:], in_=bank[7][:, 0:24])
+        for s in range(8):
+            nc.scalar.activation(out=slot(wgg, s), in_=wg1s[:], func=ACT.Copy, scale=gain_c[:, s:s + 1])
+        load_words(tabw[1], tab_words, 1)
         gather_tab(1)
-        load_cm(5)
-        load_page(4)
-        load_words(tabw[2], tab_words, 2)
-        h2_product(5)
+        load_board(4)
         h2_put(4)
+        load_words(tabw[2], tab_words, 2)
         gather_tab(2)
-
-        def w1_chunk(a, b, raw, grouped):
-            cast_w(raw, grouped)
-            quant(wq[3 * b + a], wqs[3 * b + a], grouped)
-
-        load_w(w1, 0, 0, stage[2])
-        load_cm(6)
-        load_page(5)
-        load_w(w1, 1, 0, stage[0])
-        h2_product(6)
-        h2_put(5)
-        w1_chunk(0, 0, stage[2], half[0][:])
-        for s in range(4):
-            h1_pass(s, 0, True, False)
-        load_cm(7)
-        load_page(6)
-        load_w(w1, 2, 0, stage[1])
-        h2_product(7)
-        h2_put(6)
-        w1_chunk(1, 0, stage[0], half[1][:])
-        for s in range(4):
-            h1_pass(s, 1, False, False)
+        for a in range(3):
+            w1_chunk(0, a, a, w1half[a][:] if a < 2 else hbuf[1][:].bitcast(BF16))
+            for s in range(2):
+                h1_pass(s, a, a == 0, a == 2)
         nc.sync.dma_start(idx3[:], offs3)
-        load_page(7)
+        load_board(5)
+        h2_product(5)
+        h2_put(5)
+        gelu(0)
+        gelu(1)
         nc.sync.dma_start(idx5[:], offs5)
-        load_vec(level_c, level)
-        w1_chunk(2, 0, stage[1], half[0][:])
+
+        h1_put(0)
+        h1_put(1)
+        read_pair(0)
+        w1_chunk(1, 0, 3, w1half[3][:])
+        w1_chunk(1, 1, 4, w1half[4][:])
+        w1_chunk(2, 0, 5, w1half[0][:])
+        w1_chunk(2, 1, 0, w1half[1][:])
+        w1_chunk(1, 2, 1, hbuf[0][:].bitcast(BF16))
+        load_board(6)
+        h2_product(6)
+        h2_put(6)
+        h1_group(1)
+
+        h1_put(2)
+        h1_put(3)
+        read_pair(2)
+        w3_round(0, 0, stage[1])
+        w1_chunk(3, 0, 4, w1half[3][:])
+        w1_chunk(3, 1, 5, w1half[4][:])
+        w1_chunk(2, 2, 0, hbuf[1][:].bitcast(BF16))
+        load_board(7)
+        h2_product(7)
         h2_put(7)
-        for s in range(4):
-            h1_pass(s, 2, False, True)
-            gelu(s)
+        h1_group(2)
 
-        load_w(w1, 0, 1, stage[2])
-        load_w(w1, 1, 1, stage[0])
-        load_w(w1, 2, 1, stage[1])
-        h1_put(0, wgg0)
-        h1_put(1, wgg0)
-        fetch(0)
-        fetch(1)
-        floor(0)
-        h1_put(2, wgg0)
-        floor(1)
-        h1_put(3, wgg0)
-        w1_chunk(0, 1, stage[2], half[1][:])
-        w1_chunk(1, 1, stage[0], half[0][:])
-        w1_chunk(2, 1, stage[1], as_bf16(xs[0], 1))
-        wgg1 = stage[1]
-        for t in range(PACK):
-            nc.scalar.activation(out=cols(wgg1, t), in_=cols(wg1d, t), func=ACT.Copy, scale=gain_c[:, 1, t:t + 1])
-        fetch(2)
-        fetch(3)
-        floor(2)
-        floor(3)
-        for s in range(4, 8):
-            for n, a in enumerate((2, 0, 1)):
-                h1_pass(s, a, n == 0, n == 2)
-            gelu(s)
-
+        h1_put(4)
+        h1_put(5)
         load_f4(w4_words, 0)
         load_f4(w4_words, 1)
-        load_planes_side_by_side(nc.sync, f4sraw, w4_scales)
-        load_vec(own_c, own)
-        for b in range(2):
-            deal_f4_words(b)
-            deal_f4_scales(b)
-        cast_x(0, half[1][:])
-        quant(xq[0], xqs[0], half[1][:])
-        for s in range(4, 8):
-            h1_put(s, wgg1)
-
-        w3_slot = {(0, 0): 6, (1, 0): 0, (0, 1): 1, (1, 1): 2}
-        w3_raw = {(0, 0): stage[2], (1, 0): stage[0], (0, 1): stage[2], (1, 1): stage[0]}
-        w3_half = {(0, 0): as_bf16(xs[1], 0), (1, 0): as_bf16(xs[1], 1), (0, 1): half[0][:], (1, 1): half[1][:]}
-
-        def w3_chunk(a, b):
-            load_w(w3, a, b, w3_raw[a, b])
-            cast_w(w3_raw[a, b], w3_half[a, b])
-            quant(wq[w3_slot[a, b]], wqs[w3_slot[a, b]], w3_half[a, b])
-
-        def y_pass(s, a):
-            b, t = divmod(s, PACK)
-            f8_pass(bank[4 + t], w3_slot[a, b], t, xq[a][:], xqs[a][:], a == 0, a == 1)
-            f4_pass(bank[t], s, a, xq[a][:], xqs[a][:], a == 0, a == 1)
-
-        w3_chunk(0, 0)
-        fetch(4)
-        fetch(5)
+        load_planes_side_by_side(nc.sync, f4s, w4_scales)
+        w3_round(1, 0, stage[1])
+        w3_round(0, 1, stage[2])
+        w1_chunk(3, 2, 1, as_bf16(xn[1], 256, 512))
+        w3_round(1, 1, stage[1])
+        h1_group(3)
+        read_pair(4)
         for s in range(4):
-            y_pass(s, 0)
-        w3_chunk(1, 0)
-        floor(4)
-        floor(5)
-        fetch(6)
-        fetch(7)
-        floor(6)
-        floor(7)
-        w3_chunk(0, 1)
-        w3_chunk(1, 1)
-        x1_half = as_bf16(stage[0], 0)
-        cast_x(1, x1_half)
-        quant(xq[1], xqs[1], x1_half)
+            deal(nc.sync, s)
+        x_half = [as_bf16(stage[0], 1024, 1024), as_bf16(stage[0], 0, 1024)]
+        weave(nc.scalar.copy, xd[0][:], x_half[0], 0, S)
+        deal(nc.sync, 4)
+        deal(nc.sync, 5)
 
-        def meet(s):
-            b, t = divmod(s, PACK)
-            nc.vector.scalar_tensor_tensor(out=cols(xs[b], t), in0=cols(xs[b], t), scalar=own_c[:, b, t:t + 1],
-                                           in1=bank[4 + t][:], op0=ALU.mult, op1=ALU.max)
+        h1_put(6)
+        h1_put(7)
+        late = keep.tile([P, 5 * KP], U8, name="late", tag="h_last", align_bytes=64)
+        w3_scales = {(0, 0): late[:, 0:KP], (1, 0): late[:, KP:2 * KP], (0, 1): late[:, 2 * KP:3 * KP],
+                     (1, 1): late[:, 3 * KP:4 * KP]}
+        xqs = [late[:, 4 * KP:5 * KP], xqs1[:]]
+        read_pair(6)
+        deal(nc.sync, 6)
+        deal(nc.sync, 7)
+        for a, b in ((1, 0), (0, 1), (1, 1)):
+            quant(w3_codes[a, b], w3_scales[a, b], w3_half[a, b])
+        quant(xq[0][:], xqs[0], x_half[0])
+        for c in range(4):
+            y4_pass(c, 0)
+        quant(w3_codes[0, 0], w3_scales[0, 0], w3_half[0, 0])
+        for c in range(4):
+            y_pass(c, 0)
+        weave(nc.scalar.copy, xd[1][:], x_half[1], 0, SPLIT)
+        weave(nc.vector.tensor_copy, xd[1][:], x_half[1], SPLIT, S)
+        quant(xq[1][:], xqs[1], x_half[1])
 
-        def finish(s):
-            b, t = divmod(s, PACK)
-            nc.vector.tensor_tensor(out=cols(xs[b], t), in0=bank[t][:], in1=cols(xs[b], t), op=ALU.add)
-            nc.sync.dma_start(out=rows_of(out, s), in_=cols(xs[b], t))
+        def meet(c):
+            nc.vector.scalar_tensor_tensor(out=slot(xn, c), in0=slot(xn, c), scalar=own_c[:, c:c + 1],
+                                           in1=bank[4 + c % 4][:], op0=ALU.mult, op1=ALU.max)
 
-        for s in range(4):
-            y_pass(s, 1)
+        def finish(c):
+            if c < POOL_ADDS:
+                nc.scalar.copy(out=hbuf[c][:], in_=bank[c % 4][:])
+                nc.gpsimd.tensor_tensor(out=slot(xn, c), in0=hbuf[c][:], in1=slot(xn, c), op=ALU.add)
+            else:
+                nc.vector.tensor_tensor(out=slot(xn, c), in0=bank[c % 4][:], in1=slot(xn, c), op=ALU.add)
+            nc.sync.dma_start(out=rows_of(out, c), in_=slot(xn, c))
+
+        def close(c):
+            for a in range(0 if c >= 4 else 1, 2):
+                y_pass(c, a)
+            for a in range(0 if c >= 4 else 1, 2):
+                y4_pass(c, a)
+
+        close(0)
         meet(0)
-        for s in range(8):
-            if s + 1 < 8:
-                if s + 1 >= 4:
-                    y_pass(s + 1, 0)
-                    y_pass(s + 1, 1)
-                meet(s + 1)
-            finish(s)
+        for c in range(8):
+            if c + 1 < 8:
+                if c + 1 < 4:
+                    close(c + 1)
+                if c >= 3:
+                    close(c + 1)
+                meet(c + 1)
+            finish(c)

@@ -22,7 +22,7 @@ PACK = 4
 KP = P * PACK
 GW = 256
 SPLIT = 144
-POOL_ADDS = 3
+POOL_ADDS = 4
 
 
 def tile_list_dressage_board_scores_kernel(
@@ -56,11 +56,11 @@ def tile_list_dressage_board_scores_kernel(
         v2s = [sb("v2s%d" % a, [P, S], U8) for a in range(2)]
         f4w = [sb("f4w%d" % b, [P, 2, 2 * KP], U8) for b in range(2)]
         f4s = sb("f4s", [P, 2, H], U8)
-        stage = [sb("stage%d" % i, [P, PACK * KP], F32) for i in range(3)]
-        w1half = [sb("w1half%d" % i, [P, PACK * GW], BF16) for i in range(5)]
+        stage = [sb("stage%d" % i, [P, PACK * KP], F32) for i in range(4)]
+        w1half = [sb("w1half%d" % i, [P, PACK * GW], BF16) for i in range(4)]
         w3half = [sb("w3half%d" % i, [P, PACK * KP], F32) for i in range(2)]
         w1q = [sb("w1q%d" % i, [P, 3 * GW], U32) for i in range(2)]
-        w1qs = [sb("w1qs%d" % i, [P, 3 * KP], U8) for i in range(2)]
+        w1qs = [sb("w1qs%d" % i, [P, 3 * GW], U8) for i in range(2)]
         w3q = [sb("w3q%d" % i, [P, KP], U32) for i in range(3)]
         wg1s = sb("wg1s", [P, S], F32)
         wg2s = sb("wg2s", [P, S], F32)
@@ -88,15 +88,15 @@ def tile_list_dressage_board_scores_kernel(
         def load_words(dst, words, a):
             nc.sync.dma_start(out=dst[:].bitcast(I32), in_=words[a].rearrange("p n i -> p (n i)").bitcast(I32))
 
-        def load_planes_side_by_side(eng, dst, scales):
-            for q in range(4):
+        def load_planes_side_by_side(eng, dst, scales, quadrants):
+            for q in quadrants:
                 eng.dma_start(out=dst[32 * q:32 * q + 4, :, :].bitcast(I32),
                               in_=scales[:, 4 * q:4 * q + 4, :].rearrange("a r n -> r a n").bitcast(I32))
 
         def load_planes_packed(dst, scales, passes):
             for q in range(4):
-                nc.sync.dma_start(out=dst[32 * q:32 * q + 4 * passes, :].bitcast(I32),
-                                  in_=scales[:, 4 * q:4 * q + 4, :].bitcast(I32))
+                nc.gpsimd.dma_start(out=dst[32 * q:32 * q + 4 * passes, :].bitcast(I32),
+                                    in_=scales[:, 4 * q:4 * q + 4, :].bitcast(I32))
 
         def load_f4(words, b):
             nc.sync.dma_start(out=f4w[b][:].bitcast(I32),
@@ -136,7 +136,7 @@ def tile_list_dressage_board_scores_kernel(
             nc.vector.tensor_tensor(out=hbuf[s % 2][:], in0=bank[s % 4][:], in1=cols(xn[1], s % PACK), op=ALU.mult)
 
         def h2_put(s):
-            if s + 1 < 5:
+            if s + 1 < 6:
                 h2_product(s + 1)
             nc.vector.tensor_tensor(out=page[s][:].indirect(idx4[:]), in0=hbuf[s % 2][:], in1=wg2s[:], op=ALU.mult)
 
@@ -146,7 +146,7 @@ def tile_list_dressage_board_scores_kernel(
         wgg = [w3half[1], sb("wgg1", [P, PACK * S], F32)]
 
         def w1_codes(g, a):
-            return w1q[g % 2][:, GW * a:GW * (a + 1)], w1qs[g % 2][:, KP * a:KP * a + GW]
+            return w1q[g % 2][:, GW * a:GW * (a + 1)], w1qs[g % 2][:, GW * a:GW * (a + 1)]
 
         def w1_chunk(g, a, unit, grouped):
             raw = stage[unit // 2][:, 1024 * (unit % 2):1024 * (unit % 2 + 1)]
@@ -160,6 +160,10 @@ def tile_list_dressage_board_scores_kernel(
             m = slice(P * (s % 2), P * (s % 2 + 1))
             nc.tensor.matmul_mx(out=bank[4 + s % 4][:], lhsT=codes[:, m].bitcast(FP8X4), lhsT_scale=scales[:, m],
                                 rhs=vw[a][:].bitcast(FP8X4), rhs_scale=vs[4 * a:P, :], start=start, stop=stop)
+
+        def h1_passes(g, a):
+            for s in (2 * g, 2 * g + 1):
+                h1_pass(s, a, a == 0, a == 2)
 
         def gelu(s):
             nc.scalar.activation(out=hbuf[2 + s % 2][:], in_=bank[4 + s % 4][:], func=ACT.Gelu_apprx_tanh)
@@ -210,24 +214,27 @@ def tile_list_dressage_board_scores_kernel(
         def y4_pass(c, a):
             f4_pass(bank[c % 4], c, a, xq[a][:], xqs[a])
 
+        tab2s_planes = tab2s[:].rearrange("p (a n) -> p a n", a=2)
         nc.vector.memset(tab2s[:].bitcast(I32), 0)
         nc.vector.memset(f4s[:].rearrange("p a n -> p (a n)").bitcast(I32), 0)
-        nc.vector.memset(warm[:], 0.0)
-        make_identity(nc, ident[:])
-        nc.gpsimd.memset(vec_rows[:], 0.0)
         nc.vector.memset(tabs[:].bitcast(I32), 0)
+        nc.vector.memset(warm[:], 0.0)
         nc.scalar.activation(out=warm[:], in_=warm[:], func=ACT.Gelu_apprx_tanh)
-        load_words(tab2w[0], tab2_words, 0)
-        load_planes_side_by_side(nc.sync, tab2s[:].rearrange("p (a n) -> p a n", a=2), tab2_scales)
         nc.sync.dma_start(idx2[:], offs2)
+        load_words(tab2w[0], tab2_words, 0)
+        load_planes_side_by_side(nc.sync, tab2s_planes, tab2_scales, range(4))
         load_words(tab2w[1], tab2_words, 1)
         load_f4(w2_words, 0)
-        load_planes_side_by_side(nc.sync, f4s, w2_scales)
+        load_planes_side_by_side(nc.sync, f4s, w2_scales, range(4))
+        load_planes_packed(tabs, tab_scales, 3)
+        make_identity(nc, ident[:])
+        nc.gpsimd.memset(vec_rows[:], 0.0)
         nc.sync.dma_start(out=page[0][:], in_=rows_of(page0, 0))
         load_cm(0)
         nc.sync.dma_start(out=wg2s[:], in_=wg2)
         nc.sync.dma_start(idx4[:], offs4)
         load_cm(1)
+        nc.sync.dma_start(idx1[:], offs)
 
         for a in range(2):
             nc.vector.tensor_copy(out=v2w[a][:], in_=tab2w[a][:].indirect(idx2[:]))
@@ -235,14 +242,12 @@ def tile_list_dressage_board_scores_kernel(
 
         h2_product(0)
         h2_put(0)
+        nc.vector.tensor_copy(out=vs[:], in_=tabs[:].indirect(idx1[:]))
         load_board(1)
         h2_put(1)
         load_board(2)
         h2_put(2)
-        nc.sync.dma_start(idx1[:], offs)
-        load_planes_packed(tabs, tab_scales, 3)
         load_words(tabw[0], tab_words, 0)
-        nc.vector.tensor_copy(out=vs[:], in_=tabs[:].indirect(idx1[:]))
         gather_tab(0)
         load_f4(w2_words, 1)
         load_board(3)
@@ -260,14 +265,15 @@ def tile_list_dressage_board_scores_kernel(
         h2_put(4)
         load_words(tabw[2], tab_words, 2)
         gather_tab(2)
-        for a in range(3):
-            w1_chunk(0, a, a, w1half[a][:] if a < 2 else hbuf[1][:].bitcast(BF16))
-            for s in range(2):
-                h1_pass(s, a, a == 0, a == 2)
-        nc.sync.dma_start(idx3[:], offs3)
         load_board(5)
-        h2_product(5)
         h2_put(5)
+        for a in range(3):
+            w1_chunk(0, a, a, w1half[a][:] if a < 2 else hbuf[0][:].bitcast(BF16))
+            h1_passes(0, a)
+        nc.sync.dma_start(idx3[:], offs3)
+        load_board(6)
+        h2_product(6)
+        h2_put(6)
         gelu(0)
         gelu(1)
         nc.sync.dma_start(idx5[:], offs5)
@@ -276,37 +282,42 @@ def tile_list_dressage_board_scores_kernel(
         h1_put(1)
         read_pair(0)
         w1_chunk(1, 0, 3, w1half[3][:])
-        w1_chunk(1, 1, 4, w1half[4][:])
+        w1_chunk(1, 1, 4, w1half[2][:])
         w1_chunk(2, 0, 5, w1half[0][:])
         w1_chunk(2, 1, 0, w1half[1][:])
-        w1_chunk(1, 2, 1, hbuf[0][:].bitcast(BF16))
-        load_board(6)
-        h2_product(6)
-        h2_put(6)
-        h1_group(1)
-
-        h1_put(2)
-        h1_put(3)
-        read_pair(2)
-        w3_round(0, 0, stage[1])
-        w1_chunk(3, 0, 4, w1half[3][:])
-        w1_chunk(3, 1, 5, w1half[4][:])
-        w1_chunk(2, 2, 0, hbuf[1][:].bitcast(BF16))
+        w3_round(0, 0, stage[3])
+        w1_chunk(1, 2, 1, hbuf[1][:].bitcast(BF16))
         load_board(7)
         h2_product(7)
         h2_put(7)
-        h1_group(2)
+        h1_group(1)
+        h1_passes(2, 0)
+        h1_passes(2, 1)
+
+        h1_put(2)
+        h1_put(3)
+        w1_chunk(3, 0, 2, w1half[3][:])
+        w1_chunk(3, 1, 3, w1half[2][:])
+        w1_chunk(2, 2, 0, as_bf16(xn[0], 1280, 512))
+        h1_passes(2, 2)
+        gelu(4)
+        gelu(5)
+        h1_passes(3, 0)
+        h1_passes(3, 1)
+        read_pair(2)
 
         h1_put(4)
         h1_put(5)
         load_f4(w4_words, 0)
         load_f4(w4_words, 1)
-        load_planes_side_by_side(nc.sync, f4s, w4_scales)
-        w3_round(1, 0, stage[1])
-        w3_round(0, 1, stage[2])
+        load_planes_side_by_side(nc.gpsimd, f4s, w4_scales, range(4))
+        w3_round(1, 0, stage[2])
         w1_chunk(3, 2, 1, as_bf16(xn[1], 256, 512))
+        h1_passes(3, 2)
+        gelu(6)
+        gelu(7)
+        w3_round(0, 1, stage[3])
         w3_round(1, 1, stage[1])
-        h1_group(3)
         read_pair(4)
         for s in range(4):
             deal(nc.sync, s)
@@ -324,12 +335,11 @@ def tile_list_dressage_board_scores_kernel(
         read_pair(6)
         deal(nc.sync, 6)
         deal(nc.sync, 7)
-        for a, b in ((1, 0), (0, 1), (1, 1)):
-            quant(w3_codes[a, b], w3_scales[a, b], w3_half[a, b])
         quant(xq[0][:], xqs[0], x_half[0])
         for c in range(4):
             y4_pass(c, 0)
-        quant(w3_codes[0, 0], w3_scales[0, 0], w3_half[0, 0])
+        for a, b in ((0, 0), (1, 0), (0, 1), (1, 1)):
+            quant(w3_codes[a, b], w3_scales[a, b], w3_half[a, b])
         for c in range(4):
             y_pass(c, 0)
         weave(nc.scalar.copy, xd[1][:], x_half[1], 0, SPLIT)
@@ -342,8 +352,9 @@ def tile_list_dressage_board_scores_kernel(
 
         def finish(c):
             if c < POOL_ADDS:
-                nc.scalar.copy(out=hbuf[c][:], in_=bank[c % 4][:])
-                nc.gpsimd.tensor_tensor(out=slot(xn, c), in0=hbuf[c][:], in1=slot(xn, c), op=ALU.add)
+                y4 = (hbuf[0], hbuf[1], hbuf[2], wg2s)[c]
+                nc.scalar.copy(out=y4[:], in_=bank[c % 4][:])
+                nc.gpsimd.tensor_tensor(out=slot(xn, c), in0=y4[:], in1=slot(xn, c), op=ALU.add)
             else:
                 nc.vector.tensor_tensor(out=slot(xn, c), in0=bank[c % 4][:], in1=slot(xn, c), op=ALU.add)
             nc.sync.dma_start(out=rows_of(out, c), in_=slot(xn, c))

@@ -22,7 +22,7 @@ PACK = 4
 KP = P * PACK
 GW = 256
 SPLIT = 144
-POOL_ADDS = 4
+POOL_ADDS = 3
 
 
 def tile_list_dressage_board_scores_kernel(
@@ -95,8 +95,8 @@ def tile_list_dressage_board_scores_kernel(
 
         def load_planes_packed(dst, scales, passes):
             for q in range(4):
-                nc.gpsimd.dma_start(out=dst[32 * q:32 * q + 4 * passes, :].bitcast(I32),
-                                    in_=scales[:, 4 * q:4 * q + 4, :].bitcast(I32))
+                nc.sync.dma_start(out=dst[32 * q:32 * q + 4 * passes, :].bitcast(I32),
+                                  in_=scales[:, 4 * q:4 * q + 4, :].bitcast(I32))
 
         def load_f4(words, b):
             nc.sync.dma_start(out=f4w[b][:].bitcast(I32),
@@ -226,7 +226,6 @@ def tile_list_dressage_board_scores_kernel(
         load_words(tab2w[1], tab2_words, 1)
         load_f4(w2_words, 0)
         load_planes_side_by_side(nc.sync, f4s, w2_scales, range(4))
-        load_planes_packed(tabs, tab_scales, 3)
         make_identity(nc, ident[:])
         nc.gpsimd.memset(vec_rows[:], 0.0)
         nc.sync.dma_start(out=page[0][:], in_=rows_of(page0, 0))
@@ -234,7 +233,6 @@ def tile_list_dressage_board_scores_kernel(
         nc.sync.dma_start(out=wg2s[:], in_=wg2)
         nc.sync.dma_start(idx4[:], offs4)
         load_cm(1)
-        nc.sync.dma_start(idx1[:], offs)
 
         for a in range(2):
             nc.vector.tensor_copy(out=v2w[a][:], in_=tab2w[a][:].indirect(idx2[:]))
@@ -242,12 +240,14 @@ def tile_list_dressage_board_scores_kernel(
 
         h2_product(0)
         h2_put(0)
-        nc.vector.tensor_copy(out=vs[:], in_=tabs[:].indirect(idx1[:]))
         load_board(1)
         h2_put(1)
         load_board(2)
         h2_put(2)
+        nc.sync.dma_start(idx1[:], offs)
+        load_planes_packed(tabs, tab_scales, 3)
         load_words(tabw[0], tab_words, 0)
+        nc.vector.tensor_copy(out=vs[:], in_=tabs[:].indirect(idx1[:]))
         gather_tab(0)
         load_f4(w2_words, 1)
         load_board(3)
@@ -310,7 +310,7 @@ def tile_list_dressage_board_scores_kernel(
         h1_put(5)
         load_f4(w4_words, 0)
         load_f4(w4_words, 1)
-        load_planes_side_by_side(nc.gpsimd, f4s, w4_scales, range(4))
+        load_planes_side_by_side(nc.sync, f4s, w4_scales, range(4))
         w3_round(1, 0, stage[2])
         w1_chunk(3, 2, 1, as_bf16(xn[1], 256, 512))
         h1_passes(3, 2)
@@ -352,7 +352,7 @@ def tile_list_dressage_board_scores_kernel(
 
         def finish(c):
             if c < POOL_ADDS:
-                y4 = (hbuf[0], hbuf[1], hbuf[2], wg2s)[c]
+                y4 = hbuf[c]
                 nc.scalar.copy(out=y4[:], in_=bank[c % 4][:])
                 nc.gpsimd.tensor_tensor(out=slot(xn, c), in0=y4[:], in1=slot(xn, c), op=ALU.add)
             else:

@@ -20,9 +20,14 @@ ACT = mybir.ActivationFunctionType
 P = 128
 PACK = 4
 KP = P * PACK
-GW = 256
+QUADS = 4
+SLICES = H // P
+HALF = SLICES // 2
+GROUP = 2 * P
+UNIT = PACK * GROUP
+RUN = 4
 SPLIT = 144
-POOL_ADDS = 3
+POOL_SUMS = 3
 
 
 def tile_list_dressage_board_scores_kernel(
@@ -44,334 +49,328 @@ def tile_list_dressage_board_scores_kernel(
         idx4 = lists.tile([P, S // 16], U16, name="idx4")
         idx5 = lists.tile([P, S // 16], U16, name="idx5")
 
-        bank = [psum.tile([P, S], F32, name="bank%d" % i) for i in range(8)]
-        page = [sb("page%d" % s, [P, T2], F32) for s in range(8)]
-        tabw = [sb("tabw%d" % a, [P, T], U32) for a in range(3)]
-        tab2w = [sb("tab2w%d" % a, [P, T3], U32) for a in range(2)]
-        tabs = sb("tabs", [P, T], U8)
-        tab2s = sb("tab2s", [P, 2 * T3], U8)
-        vw = [sb("vw%d" % a, [P, S], U32) for a in range(3)]
-        v2w = [sb("v2w%d" % a, [P, S], U32) for a in range(2)]
-        vs = sb("vs", [P, S], U8)
-        v2s = [sb("v2s%d" % a, [P, S], U8) for a in range(2)]
-        f4w = [sb("f4w%d" % b, [P, 2, 2 * KP], U8) for b in range(2)]
-        f4s = sb("f4s", [P, 2, H], U8)
-        stage = [sb("stage%d" % i, [P, PACK * KP], F32) for i in range(4)]
-        w1half = [sb("w1half%d" % i, [P, PACK * GW], BF16) for i in range(4)]
-        w3half = [sb("w3half%d" % i, [P, PACK * KP], F32) for i in range(2)]
-        w1q = [sb("w1q%d" % i, [P, 3 * GW], U32) for i in range(2)]
-        w1qs = [sb("w1qs%d" % i, [P, 3 * GW], U8) for i in range(2)]
-        w3q = [sb("w3q%d" % i, [P, KP], U32) for i in range(3)]
-        wg1s = sb("wg1s", [P, S], F32)
-        wg2s = sb("wg2s", [P, S], F32)
-        hbuf = [sb("hbuf%d" % i, [P, S], F32) for i in range(3)]
-        hbuf.append(keep.tile([P, S], F32, name="hbuf3", tag="h_last", align_bytes=64))
-        xn = [sb("xn%d" % b, [P, PACK * S], F32) for b in range(2)]
-        xd = [stage[2], sb("xd1", [P, PACK * S], F32)]
-        xq = [sb("xq%d" % b, [P, S], U32) for b in range(2)]
-        xqs1 = sb("xqs1", [P, S], U8)
+        bank = [psum.tile([P, S], F32, name="bank%d" % i) for i in range(SLICES)]
+        page = [sb("page%d" % s, [P, T2], F32) for s in range(SLICES)]
+        tab_w = [sb("tab_w%d" % a, [P, T], U32) for a in range(K // KP)]
+        tab2_w = [sb("tab2_w%d" % a, [P, T3], U32) for a in range(K2 // KP)]
+        tab_s = sb("tab_s", [P, T], U8)
+        tab2_s = sb("tab2_s", [P, 2 * T3], U8)
+        v_w = [sb("v_w%d" % a, [P, S], U32) for a in range(K // KP)]
+        v2_w = [sb("v2_w%d" % a, [P, S], U32) for a in range(K2 // KP)]
+        v_s = sb("v_s", [P, S], U8)
+        v2_s = [sb("v2_s%d" % a, [P, S], U8) for a in range(K2 // KP)]
+        fp4_w = [sb("fp4_w%d" % b, [P, 2, 2 * KP], U8) for b in range(2)]
+        fp4_s = sb("fp4_s", [P, 2, H], U8)
+        stage = [sb("stage%d" % i, [P, 2 * UNIT], F32) for i in range(4)]
+        w1_woven = [sb("w1_woven%d" % i, [P, UNIT], BF16) for i in range(4)]
+        w3_store = [sb("w3_store%d" % b, [P, 2 * UNIT], F32) for b in range(2)]
+        w1_w = [sb("w1_w%d" % i, [P, 3 * GROUP], U32) for i in range(2)]
+        w1_s = [sb("w1_s%d" % i, [P, 3 * GROUP], U8) for i in range(2)]
+        w3_tiles = [sb("w3_w%d" % i, [P, KP], U32) for i in range(3)]
+        wg1_sb = sb("wg1_sb", [P, S], F32)
+        wg2_sb = sb("wg2_sb", [P, S], F32)
+        h_buf = [sb("h_buf%d" % i, [P, S], F32) for i in range(3)]
+        h_buf.append(keep.tile([P, S], F32, name="h_buf3", tag="behind_last_scatter", align_bytes=64))
+        x_rows = [sb("x_rows%d" % b, [P, HALF * S], F32) for b in range(2)]
+        x_dealt = [stage[2], sb("x_dealt1", [P, PACK * S], F32)]
+        x_w = [sb("x_w%d" % a, [P, S], U32) for a in range(2)]
+        x_s1 = sb("x_s1", [P, S], U8)
         ident = sb("ident", [P, P], F32)
         vec_rows = sb("vec_rows", [P, P], F32)
-        vec_cols = sb("vec_cols", [P, 24], F32)
-        gain_c, level_c, own_c = vec_cols[:, 0:8], vec_cols[:, 8:16], vec_cols[:, 16:24]
-        warm = sb("warm", [P, 1], F32)
+        vec_cols = sb("vec_cols", [P, 3 * SLICES], F32)
+        gain_c, level_c, own_c = [vec_cols[:, SLICES * n:SLICES * (n + 1)] for n in range(3)]
+        wg1_gain = [w3_store[1], sb("wg1_gain1", [P, HALF * S], F32)]
 
         def cols(tile, t):
             return tile[:, t * S:(t + 1) * S]
 
-        def slot(pair, s):
-            return cols(pair[s // PACK], s % PACK)
+        def slice_of(pair, s):
+            return cols(pair[s // HALF], s % HALF)
 
         def rows_of(mat, s):
             return mat[P * s:P * (s + 1), :]
 
-        def load_words(dst, words, a):
-            nc.sync.dma_start(out=dst[:].bitcast(I32), in_=words[a].rearrange("p n i -> p (n i)").bitcast(I32))
-
-        def load_planes_side_by_side(eng, dst, scales, quadrants):
-            for q in quadrants:
-                eng.dma_start(out=dst[32 * q:32 * q + 4, :, :].bitcast(I32),
-                              in_=scales[:, 4 * q:4 * q + 4, :].rearrange("a r n -> r a n").bitcast(I32))
-
-        def load_planes_packed(dst, scales, passes):
-            for q in range(4):
-                nc.sync.dma_start(out=dst[32 * q:32 * q + 4 * passes, :].bitcast(I32),
-                                  in_=scales[:, 4 * q:4 * q + 4, :].bitcast(I32))
-
-        def load_f4(words, b):
-            nc.sync.dma_start(out=f4w[b][:].bitcast(I32),
-                              in_=words[:, :, 2 * KP * b:2 * KP * (b + 1)].rearrange("a p n -> p a n").bitcast(I32))
-
-        def f4_pass(acc, s, a, rhs, rhs_scale):
-            b, t = divmod(s, PACK)
-            nc.tensor.matmul_mx(out=acc[:], lhsT=f4w[b][:, a, 2 * P * t:2 * P * (t + 1)].bitcast(FP4X4),
-                                lhsT_scale=f4s[:, a, P * s:P * (s + 1)],
-                                rhs=rhs.bitcast(FP8X4), rhs_scale=rhs_scale, start=a == 0, stop=a == 1)
-
-        def load_w(w, a, lo, width, raw):
-            nc.sync.dma_start(out=raw.rearrange("p (i n) -> p i n", i=PACK),
-                              in_=w[KP * a:KP * (a + 1), lo:lo + width].rearrange("(p i) n -> p i n", i=PACK))
-
-        def weave(copy, src, grouped, lo, hi):
-            copy(out=grouped.rearrange("p (c i t) -> p c t i", i=4, t=PACK)[:, lo // 4:hi // 4, :, :],
-                 in_=src.rearrange("p (t c i) -> p c t i", t=PACK, i=4)[:, lo // 4:hi // 4, :, :])
-
-        def quant(codes, scales, grouped):
-            nc.vector.quantize_mx(out=codes.bitcast(FP8X4), scales=scales, in_=grouped)
-
         def as_bf16(tile, lo, words):
             return tile[:, lo:lo + words].bitcast(BF16)
 
-        def load_cm(s):
-            nc.sync.dma_start(out=cols(xn[1], s % PACK), in_=rows_of(cm, s))
+        def load_words(dst, words, a):
+            nc.sync.dma_start(out=dst[:].bitcast(I32), in_=words[a].rearrange("p n i -> p (n i)").bitcast(I32))
 
-        def load_board(s):
-            if s + 1 < 8:
-                load_cm(s + 1)
+        def load_planes_side_by_side(dst, scales):
+            for q in range(QUADS):
+                nc.sync.dma_start(out=dst[32 * q:32 * q + 4, :, :].bitcast(I32),
+                                  in_=scales[:, 4 * q:4 * q + 4, :].rearrange("a r n -> r a n").bitcast(I32))
+
+        def load_planes_stacked(dst, scales):
+            for q in range(QUADS):
+                nc.sync.dma_start(out=dst[32 * q:32 * q + 4 * scales.shape[0], :].bitcast(I32),
+                                  in_=scales[:, 4 * q:4 * q + 4, :].bitcast(I32))
+
+        def load_fp4(words, b):
+            nc.sync.dma_start(out=fp4_w[b][:].bitcast(I32),
+                              in_=words[:, :, 2 * KP * b:2 * KP * (b + 1)].rearrange("a p n -> p a n").bitcast(I32))
+
+        def load_cm(s):
+            nc.sync.dma_start(out=cols(x_rows[1], s % HALF), in_=rows_of(cm, s))
+
+        def load_page(s):
             nc.sync.dma_start(out=page[s][:], in_=rows_of(page0, s))
+
+        def load_pass(w, a, lo, width, raw):
+            nc.sync.dma_start(out=raw.rearrange("p (i n) -> p i n", i=PACK),
+                              in_=w[KP * a:KP * (a + 1), lo:lo + width].rearrange("(p i) n -> p i n", i=PACK))
+
+        def weave(copy, src, woven, lo, hi):
+            copy(out=woven.rearrange("p (c e i) -> p c i e", e=RUN, i=PACK)[:, lo // RUN:hi // RUN, :, :],
+                 in_=src.rearrange("p (i c e) -> p c i e", e=RUN, i=PACK)[:, lo // RUN:hi // RUN, :, :])
+
+        def quantise(words, scales, woven):
+            nc.vector.quantize_mx(out=words.bitcast(FP8X4), scales=scales, in_=woven)
+
+        def fp4_pass(s, a, rhs, rhs_scale):
+            b, t = divmod(s, HALF)
+            nc.tensor.matmul_mx(out=bank[t][:], lhsT=fp4_w[b][:, a, 2 * P * t:2 * P * (t + 1)].bitcast(FP4X4),
+                                lhsT_scale=fp4_s[:, a, P * s:P * (s + 1)],
+                                rhs=rhs.bitcast(FP8X4), rhs_scale=rhs_scale, start=a == 0, stop=a == 1)
+
+        last = SLICES - 1
 
         def h2_product(s):
             for a in range(2):
-                f4_pass(bank[s % 4], s, a, v2w[a][:], v2s[a][:])
-            nc.vector.tensor_tensor(out=hbuf[s % 2][:], in0=bank[s % 4][:], in1=cols(xn[1], s % PACK), op=ALU.mult)
+                fp4_pass(s, a, v2_w[a][:], v2_s[a][:])
+            factor, h2 = cols(x_rows[1], s % HALF), h_buf[s % 3][:]
+            if s < last:
+                nc.gpsimd.tensor_tensor(out=factor, in0=factor, in1=wg2_sb[:], op=ALU.mult)
+            if 0 < s < last:
+                nc.scalar.copy(out=h2, in_=bank[s % HALF][:])
+                nc.gpsimd.tensor_tensor(out=h2, in0=h2, in1=factor, op=ALU.mult)
+            else:
+                nc.vector.tensor_tensor(out=h2, in0=bank[s % HALF][:], in1=factor, op=ALU.mult)
 
         def h2_put(s):
-            if s + 1 < 6:
-                h2_product(s + 1)
-            nc.vector.tensor_tensor(out=page[s][:].indirect(idx4[:]), in0=hbuf[s % 2][:], in1=wg2s[:], op=ALU.mult)
+            if s < last:
+                nc.vector.tensor_copy(out=page[s][:].indirect(idx4[:]), in_=h_buf[s % 3][:])
+            else:
+                nc.vector.tensor_tensor(out=page[s][:].indirect(idx4[:]), in0=h_buf[s % 3][:], in1=wg2_sb[:],
+                                        op=ALU.mult)
+
+        def h2_step(s):
+            load_cm(s + 1)
+            load_page(s)
+            h2_product(s + 1)
+            h2_put(s)
 
         def gather_tab(a):
-            nc.vector.tensor_copy(out=vw[a][:], in_=tabw[a][:].indirect(idx1[:]))
+            load_words(tab_w[a], tab_words, a)
+            nc.vector.tensor_copy(out=v_w[a][:], in_=tab_w[a][:].indirect(idx1[:]))
 
-        wgg = [w3half[1], sb("wgg1", [P, PACK * S], F32)]
+        def w1_operand(g, a):
+            span = slice(GROUP * a, GROUP * (a + 1))
+            return w1_w[g % 2][:, span], w1_s[g % 2][:, span]
 
-        def w1_codes(g, a):
-            return w1q[g % 2][:, GW * a:GW * (a + 1)], w1qs[g % 2][:, GW * a:GW * (a + 1)]
-
-        def w1_chunk(g, a, unit, grouped):
-            raw = stage[unit // 2][:, 1024 * (unit % 2):1024 * (unit % 2 + 1)]
-            load_w(w1, a, GW * g, GW, raw)
-            weave(nc.scalar.copy, raw, grouped, 0, GW)
-            codes, scales = w1_codes(g, a)
-            quant(codes, scales, grouped)
+        def w1_chunk(g, a, unit, woven):
+            raw = stage[unit // 2][:, UNIT * (unit % 2):UNIT * (unit % 2 + 1)]
+            load_pass(w1, a, GROUP * g, GROUP, raw)
+            weave(nc.scalar.copy, raw, woven, 0, GROUP)
+            quantise(*w1_operand(g, a), woven)
 
         def h1_pass(s, a, start, stop):
-            codes, scales = w1_codes(s // 2, a)
+            words, scales = w1_operand(s // 2, a)
             m = slice(P * (s % 2), P * (s % 2 + 1))
-            nc.tensor.matmul_mx(out=bank[4 + s % 4][:], lhsT=codes[:, m].bitcast(FP8X4), lhsT_scale=scales[:, m],
-                                rhs=vw[a][:].bitcast(FP8X4), rhs_scale=vs[4 * a:P, :], start=start, stop=stop)
+            nc.tensor.matmul_mx(out=bank[HALF + s % HALF][:], lhsT=words[:, m].bitcast(FP8X4),
+                                lhsT_scale=scales[:, m], rhs=v_w[a][:].bitcast(FP8X4), rhs_scale=v_s[4 * a:P, :],
+                                start=start, stop=stop)
 
         def h1_passes(g, a):
             for s in (2 * g, 2 * g + 1):
                 h1_pass(s, a, a == 0, a == 2)
 
         def gelu(s):
-            nc.scalar.activation(out=hbuf[2 + s % 2][:], in_=bank[4 + s % 4][:], func=ACT.Gelu_apprx_tanh)
+            nc.scalar.activation(out=h_buf[2 + s % 2][:], in_=bank[HALF + s % HALF][:], func=ACT.Gelu_apprx_tanh)
 
-        def h1_group(g):
+        def h1_put(g):
             for s in (2 * g, 2 * g + 1):
-                for n, a in enumerate((2, 0, 1)):
-                    h1_pass(s, a, n == 0, n == 2)
-                gelu(s)
+                nc.vector.tensor_tensor(out=page[s][:].indirect(idx3[:]), in0=h_buf[2 + s % 2][:],
+                                        in1=slice_of(wg1_gain, s), op=ALU.mult)
 
-        def h1_put(s):
-            nc.vector.tensor_tensor(out=page[s][:].indirect(idx3[:]), in0=hbuf[2 + s % 2][:],
-                                    in1=slot(wgg, s), op=ALU.mult)
+        def read_page(g):
+            for s in (2 * g, 2 * g + 1):
+                nc.vector.tensor_copy(out=slice_of(x_rows, s), in_=page[s][:].indirect(idx5[:]))
+            for s in (2 * g, 2 * g + 1):
+                nc.vector.tensor_scalar(out=slice_of(x_rows, s), in0=slice_of(x_rows, s),
+                                        scalar1=level_c[:, s:s + 1], scalar2=None, op0=ALU.max)
 
-        def fetch(s):
-            nc.vector.tensor_copy(out=slot(xn, s), in_=page[s][:].indirect(idx5[:]))
+        def deal(s):
+            a, q = divmod(s, HALF)
+            for i in range(PACK):
+                nc.sync.dma_start(out=cols(x_dealt[a], i)[32 * q:32 * (q + 1), :],
+                                  in_=slice_of(x_rows, s)[i:P:PACK, :])
 
-        def floor(s):
-            nc.vector.tensor_scalar(out=slot(xn, s), in0=slot(xn, s), scalar1=level_c[:, s:s + 1],
-                                    scalar2=None, op0=ALU.max)
+        w3_order = [(a, b) for b in range(2) for a in range(2)]
+        w3_w = dict(zip(w3_order, [tile[:] for tile in w3_tiles] + [w1_w[1][:, 0:KP]]))
+        w3_woven = {(a, b): as_bf16(w3_store[b], UNIT * a, UNIT) for a, b in w3_order}
 
-        def deal(eng, s):
-            b, q = divmod(s, PACK)
-            for t in range(PACK):
-                eng.dma_start(out=cols(xd[b], t)[32 * q:32 * (q + 1), :], in_=slot(xn, s)[t:P:PACK, :])
+        def w3_chunk(a, b, raw):
+            load_pass(w3, a, KP * b, KP, raw[:])
+            weave(nc.scalar.copy, raw[:], w3_woven[a, b], 0, KP)
 
-        def read_pair(s):
-            fetch(s)
-            fetch(s + 1)
-            floor(s)
-            floor(s + 1)
-
-        w3_codes = {(0, 0): w3q[0][:], (1, 0): w3q[1][:], (0, 1): w3q[2][:], (1, 1): w1q[1][:, 0:KP]}
-        w3_half = {(0, 0): as_bf16(w3half[0], 0, 1024), (1, 0): as_bf16(w3half[0], 1024, 1024),
-                   (0, 1): as_bf16(w3half[1], 0, 1024), (1, 1): as_bf16(w3half[1], 1024, 1024)}
-
-        def w3_round(a, b, raw):
-            load_w(w3, a, KP * b, KP, raw[:])
-            weave(nc.scalar.copy, raw[:], w3_half[a, b], 0, KP)
-
-        def y_pass(c, a):
-            b, t = divmod(c, PACK)
-            m = slice(P * t, P * (t + 1))
-            nc.tensor.matmul_mx(out=bank[4 + t][:], lhsT=w3_codes[a, b][:, m].bitcast(FP8X4),
-                                lhsT_scale=w3_scales[a, b][:, m],
-                                rhs=xq[a][:].bitcast(FP8X4), rhs_scale=xqs[a], start=a == 0, stop=a == 1)
-
-        def y4_pass(c, a):
-            f4_pass(bank[c % 4], c, a, xq[a][:], xqs[a])
-
-        tab2s_planes = tab2s[:].rearrange("p (a n) -> p a n", a=2)
-        nc.vector.memset(tab2s[:].bitcast(I32), 0)
-        nc.vector.memset(f4s[:].rearrange("p a n -> p (a n)").bitcast(I32), 0)
-        nc.vector.memset(tabs[:].bitcast(I32), 0)
-        nc.vector.memset(warm[:], 0.0)
-        nc.scalar.activation(out=warm[:], in_=warm[:], func=ACT.Gelu_apprx_tanh)
+        nc.vector.memset(tab2_s[:].bitcast(I32), 0)
+        nc.vector.memset(fp4_s[:].rearrange("p a n -> p (a n)").bitcast(I32), 0)
+        nc.vector.memset(tab_s[:].bitcast(I32), 0)
         nc.sync.dma_start(idx2[:], offs2)
-        load_words(tab2w[0], tab2_words, 0)
-        load_planes_side_by_side(nc.sync, tab2s_planes, tab2_scales, range(4))
-        load_words(tab2w[1], tab2_words, 1)
-        load_f4(w2_words, 0)
-        load_planes_side_by_side(nc.sync, f4s, w2_scales, range(4))
+        load_words(tab2_w[0], tab2_words, 0)
+        load_planes_side_by_side(tab2_s[:].rearrange("p (a n) -> p a n", a=2), tab2_scales)
+        load_words(tab2_w[1], tab2_words, 1)
+        load_fp4(w2_words, 0)
+        load_planes_side_by_side(fp4_s, w2_scales)
         make_identity(nc, ident[:])
         nc.gpsimd.memset(vec_rows[:], 0.0)
-        nc.sync.dma_start(out=page[0][:], in_=rows_of(page0, 0))
         load_cm(0)
-        nc.sync.dma_start(out=wg2s[:], in_=wg2)
+        nc.sync.dma_start(out=wg2_sb[:], in_=wg2)
+        load_page(0)
         nc.sync.dma_start(idx4[:], offs4)
         load_cm(1)
-
         for a in range(2):
-            nc.vector.tensor_copy(out=v2w[a][:], in_=tab2w[a][:].indirect(idx2[:]))
-            nc.vector.tensor_copy(out=v2s[a][:], in_=tab2s[:, T3 * a:T3 * (a + 1)].indirect(idx2[:]))
-
+            nc.vector.tensor_copy(out=v2_w[a][:], in_=tab2_w[a][:].indirect(idx2[:]))
+            nc.vector.tensor_copy(out=v2_s[a][:], in_=tab2_s[:, T3 * a:T3 * (a + 1)].indirect(idx2[:]))
         h2_product(0)
+        h2_product(1)
         h2_put(0)
-        load_board(1)
-        h2_put(1)
-        load_board(2)
-        h2_put(2)
+
+        h2_step(1)
+        h2_step(2)
         nc.sync.dma_start(idx1[:], offs)
-        load_planes_packed(tabs, tab_scales, 3)
-        load_words(tabw[0], tab_words, 0)
-        nc.vector.tensor_copy(out=vs[:], in_=tabs[:].indirect(idx1[:]))
-        gather_tab(0)
-        load_f4(w2_words, 1)
-        load_board(3)
-        h2_put(3)
-        nc.sync.dma_start(out=wg1s[:], in_=wg1)
+        load_planes_stacked(tab_s, tab_scales)
+        load_words(tab_w[0], tab_words, 0)
+        nc.vector.tensor_copy(out=v_s[:], in_=tab_s[:].indirect(idx1[:]))
+        nc.vector.tensor_copy(out=v_w[0][:], in_=tab_w[0][:].indirect(idx1[:]))
+        load_fp4(w2_words, 1)
+        h2_step(3)
         for n, vec in enumerate((gain, level, own)):
-            nc.sync.dma_start(out=vec_rows[8 * n:8 * (n + 1), :], in_=vec.rearrange("(s p) -> s p", p=P))
-        nc.tensor.transpose(bank[7][:, 0:P], vec_rows[:], ident[:])
-        nc.scalar.copy(out=vec_cols[:], in_=bank[7][:, 0:24])
-        for s in range(8):
-            nc.scalar.activation(out=slot(wgg, s), in_=wg1s[:], func=ACT.Copy, scale=gain_c[:, s:s + 1])
-        load_words(tabw[1], tab_words, 1)
+            nc.sync.dma_start(out=vec_rows[SLICES * n:SLICES * (n + 1), :], in_=vec.rearrange("(s p) -> s p", p=P))
+        nc.tensor.transpose(bank[last][:, 0:P], vec_rows[:], ident[:])
+        nc.scalar.copy(out=vec_cols[:], in_=bank[last][:, 0:3 * SLICES])
         gather_tab(1)
-        load_board(4)
-        h2_put(4)
-        load_words(tabw[2], tab_words, 2)
+        h2_step(4)
         gather_tab(2)
-        load_board(5)
-        h2_put(5)
+        h2_step(5)
+
         for a in range(3):
-            w1_chunk(0, a, a, w1half[a][:] if a < 2 else hbuf[0][:].bitcast(BF16))
+            w1_chunk(0, a, a, w1_woven[a][:])
             h1_passes(0, a)
+        load_page(6)
+        nc.sync.dma_start(out=wg1_sb[:], in_=wg1)
         nc.sync.dma_start(idx3[:], offs3)
-        load_board(6)
-        h2_product(6)
+        load_cm(last)
         h2_put(6)
         gelu(0)
         gelu(1)
+        for s in range(SLICES):
+            nc.scalar.activation(out=slice_of(wg1_gain, s), in_=wg1_sb[:], func=ACT.Copy, scale=gain_c[:, s:s + 1])
         nc.sync.dma_start(idx5[:], offs5)
-
         h1_put(0)
-        h1_put(1)
-        read_pair(0)
-        w1_chunk(1, 0, 3, w1half[3][:])
-        w1_chunk(1, 1, 4, w1half[2][:])
-        w1_chunk(2, 0, 5, w1half[0][:])
-        w1_chunk(2, 1, 0, w1half[1][:])
-        w3_round(0, 0, stage[3])
-        w1_chunk(1, 2, 1, hbuf[1][:].bitcast(BF16))
-        load_board(7)
-        h2_product(7)
-        h2_put(7)
-        h1_group(1)
+        read_page(0)
+
+        w1_chunk(1, 0, 3, w1_woven[3][:])
+        w1_chunk(1, 1, 4, w1_woven[2][:])
+        w1_chunk(2, 0, 5, w1_woven[0][:])
+        w1_chunk(2, 1, 0, w1_woven[1][:])
+        w3_chunk(0, 0, stage[3])
+        w1_chunk(1, 2, 1, h_buf[last % 3][:].bitcast(BF16))
+        load_page(last)
+        h2_product(last)
+        h2_put(last)
+        for s in (2, 3):
+            for n, a in enumerate((2, 0, 1)):
+                h1_pass(s, a, n == 0, n == 2)
+            gelu(s)
         h1_passes(2, 0)
         h1_passes(2, 1)
+        h1_put(1)
 
-        h1_put(2)
-        h1_put(3)
-        w1_chunk(3, 0, 2, w1half[3][:])
-        w1_chunk(3, 1, 3, w1half[2][:])
-        w1_chunk(2, 2, 0, as_bf16(xn[0], 1280, 512))
+        def across_x_slices(g):
+            return as_bf16(x_rows[g // 2], 2 * S * (g % 2) + S // 2, S)
+
+        w1_chunk(3, 0, 2, w1_woven[3][:])
+        w1_chunk(3, 1, 3, w1_woven[2][:])
+        w1_chunk(2, 2, 0, across_x_slices(1))
         h1_passes(2, 2)
         gelu(4)
         gelu(5)
         h1_passes(3, 0)
         h1_passes(3, 1)
-        read_pair(2)
+        read_page(1)
+        h1_put(2)
 
-        h1_put(4)
-        h1_put(5)
-        load_f4(w4_words, 0)
-        load_f4(w4_words, 1)
-        load_planes_side_by_side(nc.sync, f4s, w4_scales, range(4))
-        w3_round(1, 0, stage[2])
-        w1_chunk(3, 2, 1, as_bf16(xn[1], 256, 512))
+        load_fp4(w4_words, 0)
+        load_fp4(w4_words, 1)
+        load_planes_side_by_side(fp4_s, w4_scales)
+        w3_chunk(1, 0, stage[2])
+        w1_chunk(3, 2, 1, across_x_slices(2))
         h1_passes(3, 2)
         gelu(6)
         gelu(7)
-        w3_round(0, 1, stage[3])
-        w3_round(1, 1, stage[1])
-        read_pair(4)
-        for s in range(4):
-            deal(nc.sync, s)
-        x_half = [as_bf16(stage[0], 1024, 1024), as_bf16(stage[0], 0, 1024)]
-        weave(nc.scalar.copy, xd[0][:], x_half[0], 0, S)
-        deal(nc.sync, 4)
-        deal(nc.sync, 5)
+        w3_chunk(0, 1, stage[3])
+        w3_chunk(1, 1, stage[1])
+        read_page(2)
+        for s in range(HALF):
+            deal(s)
+        x_woven = [as_bf16(stage[0], UNIT, UNIT), as_bf16(stage[0], 0, UNIT)]
+        weave(nc.scalar.copy, x_dealt[0][:], x_woven[0], 0, S)
+        deal(4)
+        deal(5)
+        h1_put(3)
 
-        h1_put(6)
-        h1_put(7)
-        late = keep.tile([P, 5 * KP], U8, name="late", tag="h_last", align_bytes=64)
-        w3_scales = {(0, 0): late[:, 0:KP], (1, 0): late[:, KP:2 * KP], (0, 1): late[:, 2 * KP:3 * KP],
-                     (1, 1): late[:, 3 * KP:4 * KP]}
-        xqs = [late[:, 4 * KP:5 * KP], xqs1[:]]
-        read_pair(6)
-        deal(nc.sync, 6)
-        deal(nc.sync, 7)
-        quant(xq[0][:], xqs[0], x_half[0])
-        for c in range(4):
-            y4_pass(c, 0)
-        for a, b in ((0, 0), (1, 0), (0, 1), (1, 1)):
-            quant(w3_codes[a, b], w3_scales[a, b], w3_half[a, b])
-        for c in range(4):
-            y_pass(c, 0)
-        weave(nc.scalar.copy, xd[1][:], x_half[1], 0, SPLIT)
-        weave(nc.vector.tensor_copy, xd[1][:], x_half[1], SPLIT, S)
-        quant(xq[1][:], xqs[1], x_half[1])
+        late_s = keep.tile([P, 5 * KP], U8, name="late_s", tag="behind_last_scatter", align_bytes=64)
+        w3_s = {chunk: late_s[:, KP * n:KP * (n + 1)] for n, chunk in enumerate(w3_order)}
+        x_s = [late_s[:, 4 * KP:5 * KP], x_s1[:]]
 
-        def meet(c):
-            nc.vector.scalar_tensor_tensor(out=slot(xn, c), in0=slot(xn, c), scalar=own_c[:, c:c + 1],
-                                           in1=bank[4 + c % 4][:], op0=ALU.mult, op1=ALU.max)
+        def w3_pass(s, a):
+            b, t = divmod(s, HALF)
+            m = slice(P * t, P * (t + 1))
+            nc.tensor.matmul_mx(out=bank[HALF + t][:], lhsT=w3_w[a, b][:, m].bitcast(FP8X4),
+                                lhsT_scale=w3_s[a, b][:, m], rhs=x_w[a][:].bitcast(FP8X4), rhs_scale=x_s[a],
+                                start=a == 0, stop=a == 1)
 
-        def finish(c):
-            if c < POOL_ADDS:
-                y4 = hbuf[c]
-                nc.scalar.copy(out=y4[:], in_=bank[c % 4][:])
-                nc.gpsimd.tensor_tensor(out=slot(xn, c), in0=y4[:], in1=slot(xn, c), op=ALU.add)
+        read_page(3)
+        deal(6)
+        deal(7)
+        quantise(x_w[0][:], x_s[0], x_woven[0])
+        for s in range(HALF):
+            fp4_pass(s, 0, x_w[0][:], x_s[0])
+        for chunk in w3_order:
+            quantise(w3_w[chunk], w3_s[chunk], w3_woven[chunk])
+        for s in range(HALF):
+            w3_pass(s, 0)
+        weave(nc.scalar.copy, x_dealt[1][:], x_woven[1], 0, SPLIT)
+        weave(nc.vector.tensor_copy, x_dealt[1][:], x_woven[1], SPLIT, S)
+        quantise(x_w[1][:], x_s[1], x_woven[1])
+
+        def products(s):
+            todo = range(1 if s < HALF else 0, 2)
+            for a in todo:
+                w3_pass(s, a)
+            for a in todo:
+                fp4_pass(s, a, x_w[a][:], x_s[a])
+
+        def meet(s):
+            nc.vector.scalar_tensor_tensor(out=slice_of(x_rows, s), in0=slice_of(x_rows, s),
+                                           scalar=own_c[:, s:s + 1], in1=bank[HALF + s % HALF][:],
+                                           op0=ALU.mult, op1=ALU.max)
+
+        def finish(s):
+            best = slice_of(x_rows, s)
+            if s < POOL_SUMS:
+                nc.scalar.copy(out=h_buf[s][:], in_=bank[s][:])
+                nc.gpsimd.tensor_tensor(out=best, in0=h_buf[s][:], in1=best, op=ALU.add)
             else:
-                nc.vector.tensor_tensor(out=slot(xn, c), in0=bank[c % 4][:], in1=slot(xn, c), op=ALU.add)
-            nc.sync.dma_start(out=rows_of(out, c), in_=slot(xn, c))
+                nc.vector.tensor_tensor(out=best, in0=bank[s % HALF][:], in1=best, op=ALU.add)
+            nc.sync.dma_start(out=rows_of(out, s), in_=best)
 
-        def close(c):
-            for a in range(0 if c >= 4 else 1, 2):
-                y_pass(c, a)
-            for a in range(0 if c >= 4 else 1, 2):
-                y4_pass(c, a)
-
-        close(0)
+        products(0)
         meet(0)
-        for c in range(8):
-            if c + 1 < 8:
-                if c + 1 < 4:
-                    close(c + 1)
-                if c >= 3:
-                    close(c + 1)
-                meet(c + 1)
-            finish(c)
+        for s in range(last):
+            products(s + 1)
+            meet(s + 1)
+            finish(s)
+        finish(last)

from contextlib import ExitStack

import concourse.mybir as mybir
from concourse.masks import make_identity

K, K2, T, T3, S, H, T2 = 1536, 1024, 2048, 1024, 512, 1024, 2048
FLOPS = 2 * S * H * (K + K2 + H + H)

F32 = mybir.dt.float32
BF16 = mybir.dt.bfloat16
I32 = mybir.dt.int32
U32 = mybir.dt.uint32
U16 = mybir.dt.uint16
U8 = mybir.dt.uint8
FP8X4 = mybir.dt.float8_e4m3fn_x4
FP4X4 = mybir.dt.float4_e2m1fn_x4
ALU = mybir.AluOpType
ACT = mybir.ActivationFunctionType

P = 128
PACK = 4
KP = P * PACK
QUADS = 4
SLICES = H // P
HALF = SLICES // 2
GROUP = 2 * P
UNIT = PACK * GROUP
RUN = 4
SPLIT = 144
POOL_SUMS = 3


def tile_list_dressage_board_scores_kernel(
    tc, tab_words, tab_scales, tab2_words, tab2_scales, offs, offs2, offs3, offs4, offs5, w1, gain,
    w2_words, w2_scales, cm, wg1, wg2, page0, level, w3, own, w4_words, w4_scales, out,
):
    nc = tc.nc
    with ExitStack() as ctx:
        lists = ctx.enter_context(tc.tile_pool(name="lists", bufs=1))
        keep = ctx.enter_context(tc.tile_pool(name="keep", bufs=1))
        psum = ctx.enter_context(tc.psum_pool(name="psum", bufs=1))

        def sb(name, shape, dtype):
            return keep.tile(shape, dtype, name=name, align_bytes=64)

        idx1 = lists.tile([P, S // 16], U16, name="idx1")
        idx2 = lists.tile([P, S // 16], U16, name="idx2")
        idx3 = lists.tile([P, S // 16], U16, name="idx3")
        idx4 = lists.tile([P, S // 16], U16, name="idx4")
        idx5 = lists.tile([P, S // 16], U16, name="idx5")

        bank = [psum.tile([P, S], F32, name="bank%d" % i) for i in range(SLICES)]
        page = [sb("page%d" % s, [P, T2], F32) for s in range(SLICES)]
        tab_w = [sb("tab_w%d" % a, [P, T], U32) for a in range(K // KP)]
        tab2_w = [sb("tab2_w%d" % a, [P, T3], U32) for a in range(K2 // KP)]
        tab_s = sb("tab_s", [P, T], U8)
        tab2_s = sb("tab2_s", [P, 2 * T3], U8)
        v_w = [sb("v_w%d" % a, [P, S], U32) for a in range(K // KP)]
        v2_w = [sb("v2_w%d" % a, [P, S], U32) for a in range(K2 // KP)]
        v_s = sb("v_s", [P, S], U8)
        v2_s = [sb("v2_s%d" % a, [P, S], U8) for a in range(K2 // KP)]
        fp4_w = [sb("fp4_w%d" % b, [P, 2, 2 * KP], U8) for b in range(2)]
        fp4_s = sb("fp4_s", [P, 2, H], U8)
        stage = [sb("stage%d" % i, [P, 2 * UNIT], F32) for i in range(4)]
        w1_woven = [sb("w1_woven%d" % i, [P, UNIT], BF16) for i in range(4)]
        w3_store = [sb("w3_store%d" % b, [P, 2 * UNIT], F32) for b in range(2)]
        w1_w = [sb("w1_w%d" % i, [P, 3 * GROUP], U32) for i in range(2)]
        w1_s = [sb("w1_s%d" % i, [P, 3 * GROUP], U8) for i in range(2)]
        w3_tiles = [sb("w3_w%d" % i, [P, KP], U32) for i in range(3)]
        wg1_sb = sb("wg1_sb", [P, S], F32)
        wg2_sb = sb("wg2_sb", [P, S], F32)
        h_buf = [sb("h_buf%d" % i, [P, S], F32) for i in range(3)]
        h_buf.append(keep.tile([P, S], F32, name="h_buf3", tag="behind_last_scatter", align_bytes=64))
        x_rows = [sb("x_rows%d" % b, [P, HALF * S], F32) for b in range(2)]
        x_dealt = [stage[2], sb("x_dealt1", [P, PACK * S], F32)]
        x_w = [sb("x_w%d" % a, [P, S], U32) for a in range(2)]
        x_s1 = sb("x_s1", [P, S], U8)
        ident = sb("ident", [P, P], F32)
        vec_rows = sb("vec_rows", [P, P], F32)
        vec_cols = sb("vec_cols", [P, 3 * SLICES], F32)
        gain_c, level_c, own_c = [vec_cols[:, SLICES * n:SLICES * (n + 1)] for n in range(3)]
        wg1_gain = [w3_store[1], sb("wg1_gain1", [P, HALF * S], F32)]

        def cols(tile, t):
            return tile[:, t * S:(t + 1) * S]

        def slice_of(pair, s):
            return cols(pair[s // HALF], s % HALF)

        def rows_of(mat, s):
            return mat[P * s:P * (s + 1), :]

        def as_bf16(tile, lo, words):
            return tile[:, lo:lo + words].bitcast(BF16)

        def load_words(dst, words, a):
            nc.sync.dma_start(out=dst[:].bitcast(I32), in_=words[a].rearrange("p n i -> p (n i)").bitcast(I32))

        def load_planes_side_by_side(dst, scales):
            for q in range(QUADS):
                nc.sync.dma_start(out=dst[32 * q:32 * q + 4, :, :].bitcast(I32),
                                  in_=scales[:, 4 * q:4 * q + 4, :].rearrange("a r n -> r a n").bitcast(I32))

        def load_planes_stacked(dst, scales):
            for q in range(QUADS):
                nc.sync.dma_start(out=dst[32 * q:32 * q + 4 * scales.shape[0], :].bitcast(I32),
                                  in_=scales[:, 4 * q:4 * q + 4, :].bitcast(I32))

        def load_fp4(words, b):
            nc.sync.dma_start(out=fp4_w[b][:].bitcast(I32),
                              in_=words[:, :, 2 * KP * b:2 * KP * (b + 1)].rearrange("a p n -> p a n").bitcast(I32))

        def load_cm(s):
            nc.sync.dma_start(out=cols(x_rows[1], s % HALF), in_=rows_of(cm, s))

        def load_page(s):
            nc.sync.dma_start(out=page[s][:], in_=rows_of(page0, s))

        def load_pass(w, a, lo, width, raw):
            nc.sync.dma_start(out=raw.rearrange("p (i n) -> p i n", i=PACK),
                              in_=w[KP * a:KP * (a + 1), lo:lo + width].rearrange("(p i) n -> p i n", i=PACK))

        def weave(copy, src, woven, lo, hi):
            copy(out=woven.rearrange("p (c e i) -> p c i e", e=RUN, i=PACK)[:, lo // RUN:hi // RUN, :, :],
                 in_=src.rearrange("p (i c e) -> p c i e", e=RUN, i=PACK)[:, lo // RUN:hi // RUN, :, :])

        def quantise(words, scales, woven):
            nc.vector.quantize_mx(out=words.bitcast(FP8X4), scales=scales, in_=woven)

        def fp4_pass(s, a, rhs, rhs_scale):
            b, t = divmod(s, HALF)
            nc.tensor.matmul_mx(out=bank[t][:], lhsT=fp4_w[b][:, a, 2 * P * t:2 * P * (t + 1)].bitcast(FP4X4),
                                lhsT_scale=fp4_s[:, a, P * s:P * (s + 1)],
                                rhs=rhs.bitcast(FP8X4), rhs_scale=rhs_scale, start=a == 0, stop=a == 1)

        last = SLICES - 1

        def h2_product(s):
            for a in range(2):
                fp4_pass(s, a, v2_w[a][:], v2_s[a][:])
            factor, h2 = cols(x_rows[1], s % HALF), h_buf[s % 3][:]
            if s < last:
                nc.gpsimd.tensor_tensor(out=factor, in0=factor, in1=wg2_sb[:], op=ALU.mult)
            if 0 < s < last:
                nc.scalar.copy(out=h2, in_=bank[s % HALF][:])
                nc.gpsimd.tensor_tensor(out=h2, in0=h2, in1=factor, op=ALU.mult)
            else:
                nc.vector.tensor_tensor(out=h2, in0=bank[s % HALF][:], in1=factor, op=ALU.mult)

        def h2_put(s):
            if s < last:
                nc.vector.tensor_copy(out=page[s][:].indirect(idx4[:]), in_=h_buf[s % 3][:])
            else:
                nc.vector.tensor_tensor(out=page[s][:].indirect(idx4[:]), in0=h_buf[s % 3][:], in1=wg2_sb[:],
                                        op=ALU.mult)

        def h2_step(s):
            load_cm(s + 1)
            load_page(s)
            h2_product(s + 1)
            h2_put(s)

        def gather_tab(a):
            load_words(tab_w[a], tab_words, a)
            nc.vector.tensor_copy(out=v_w[a][:], in_=tab_w[a][:].indirect(idx1[:]))

        def w1_operand(g, a):
            span = slice(GROUP * a, GROUP * (a + 1))
            return w1_w[g % 2][:, span], w1_s[g % 2][:, span]

        def w1_chunk(g, a, unit, woven):
            raw = stage[unit // 2][:, UNIT * (unit % 2):UNIT * (unit % 2 + 1)]
            load_pass(w1, a, GROUP * g, GROUP, raw)
            weave(nc.scalar.copy, raw, woven, 0, GROUP)
            quantise(*w1_operand(g, a), woven)

        def h1_pass(s, a, start, stop):
            words, scales = w1_operand(s // 2, a)
            m = slice(P * (s % 2), P * (s % 2 + 1))
            nc.tensor.matmul_mx(out=bank[HALF + s % HALF][:], lhsT=words[:, m].bitcast(FP8X4),
                                lhsT_scale=scales[:, m], rhs=v_w[a][:].bitcast(FP8X4), rhs_scale=v_s[4 * a:P, :],
                                start=start, stop=stop)

        def h1_passes(g, a):
            for s in (2 * g, 2 * g + 1):
                h1_pass(s, a, a == 0, a == 2)

        def gelu(s):
            nc.scalar.activation(out=h_buf[2 + s % 2][:], in_=bank[HALF + s % HALF][:], func=ACT.Gelu_apprx_tanh)

        def h1_put(g):
            for s in (2 * g, 2 * g + 1):
                nc.vector.tensor_tensor(out=page[s][:].indirect(idx3[:]), in0=h_buf[2 + s % 2][:],
                                        in1=slice_of(wg1_gain, s), op=ALU.mult)

        def read_page(g):
            for s in (2 * g, 2 * g + 1):
                nc.vector.tensor_copy(out=slice_of(x_rows, s), in_=page[s][:].indirect(idx5[:]))
            for s in (2 * g, 2 * g + 1):
                nc.vector.tensor_scalar(out=slice_of(x_rows, s), in0=slice_of(x_rows, s),
                                        scalar1=level_c[:, s:s + 1], scalar2=None, op0=ALU.max)

        def deal(s):
            a, q = divmod(s, HALF)
            for i in range(PACK):
                nc.sync.dma_start(out=cols(x_dealt[a], i)[32 * q:32 * (q + 1), :],
                                  in_=slice_of(x_rows, s)[i:P:PACK, :])

        w3_order = [(a, b) for b in range(2) for a in range(2)]
        w3_w = dict(zip(w3_order, [tile[:] for tile in w3_tiles] + [w1_w[1][:, 0:KP]]))
        w3_woven = {(a, b): as_bf16(w3_store[b], UNIT * a, UNIT) for a, b in w3_order}

        def w3_chunk(a, b, raw):
            load_pass(w3, a, KP * b, KP, raw[:])
            weave(nc.scalar.copy, raw[:], w3_woven[a, b], 0, KP)

        nc.vector.memset(tab2_s[:].bitcast(I32), 0)
        nc.vector.memset(fp4_s[:].rearrange("p a n -> p (a n)").bitcast(I32), 0)
        nc.vector.memset(tab_s[:].bitcast(I32), 0)
        nc.sync.dma_start(idx2[:], offs2)
        load_words(tab2_w[0], tab2_words, 0)
        load_planes_side_by_side(tab2_s[:].rearrange("p (a n) -> p a n", a=2), tab2_scales)
        load_words(tab2_w[1], tab2_words, 1)
        load_fp4(w2_words, 0)
        load_planes_side_by_side(fp4_s, w2_scales)
        make_identity(nc, ident[:])
        nc.gpsimd.memset(vec_rows[:], 0.0)
        load_cm(0)
        nc.sync.dma_start(out=wg2_sb[:], in_=wg2)
        load_page(0)
        nc.sync.dma_start(idx4[:], offs4)
        load_cm(1)
        for a in range(2):
            nc.vector.tensor_copy(out=v2_w[a][:], in_=tab2_w[a][:].indirect(idx2[:]))
            nc.vector.tensor_copy(out=v2_s[a][:], in_=tab2_s[:, T3 * a:T3 * (a + 1)].indirect(idx2[:]))
        h2_product(0)
        h2_product(1)
        h2_put(0)

        h2_step(1)
        h2_step(2)
        nc.sync.dma_start(idx1[:], offs)
        load_planes_stacked(tab_s, tab_scales)
        load_words(tab_w[0], tab_words, 0)
        nc.vector.tensor_copy(out=v_s[:], in_=tab_s[:].indirect(idx1[:]))
        nc.vector.tensor_copy(out=v_w[0][:], in_=tab_w[0][:].indirect(idx1[:]))
        load_fp4(w2_words, 1)
        h2_step(3)
        for n, vec in enumerate((gain, level, own)):
            nc.sync.dma_start(out=vec_rows[SLICES * n:SLICES * (n + 1), :], in_=vec.rearrange("(s p) -> s p", p=P))
        nc.tensor.transpose(bank[last][:, 0:P], vec_rows[:], ident[:])
        nc.scalar.copy(out=vec_cols[:], in_=bank[last][:, 0:3 * SLICES])
        gather_tab(1)
        h2_step(4)
        gather_tab(2)
        h2_step(5)

        for a in range(3):
            w1_chunk(0, a, a, w1_woven[a][:])
            h1_passes(0, a)
        load_page(6)
        nc.sync.dma_start(out=wg1_sb[:], in_=wg1)
        nc.sync.dma_start(idx3[:], offs3)
        load_cm(last)
        h2_put(6)
        gelu(0)
        gelu(1)
        for s in range(SLICES):
            nc.scalar.activation(out=slice_of(wg1_gain, s), in_=wg1_sb[:], func=ACT.Copy, scale=gain_c[:, s:s + 1])
        nc.sync.dma_start(idx5[:], offs5)
        h1_put(0)
        read_page(0)

        w1_chunk(1, 0, 3, w1_woven[3][:])
        w1_chunk(1, 1, 4, w1_woven[2][:])
        w1_chunk(2, 0, 5, w1_woven[0][:])
        w1_chunk(2, 1, 0, w1_woven[1][:])
        w3_chunk(0, 0, stage[3])
        w1_chunk(1, 2, 1, h_buf[last % 3][:].bitcast(BF16))
        load_page(last)
        h2_product(last)
        h2_put(last)
        for s in (2, 3):
            for n, a in enumerate((2, 0, 1)):
                h1_pass(s, a, n == 0, n == 2)
            gelu(s)
        h1_passes(2, 0)
        h1_passes(2, 1)
        h1_put(1)

        def across_x_slices(g):
            return as_bf16(x_rows[g // 2], 2 * S * (g % 2) + S // 2, S)

        w1_chunk(3, 0, 2, w1_woven[3][:])
        w1_chunk(3, 1, 3, w1_woven[2][:])
        w1_chunk(2, 2, 0, across_x_slices(1))
        h1_passes(2, 2)
        gelu(4)
        gelu(5)
        h1_passes(3, 0)
        h1_passes(3, 1)
        read_page(1)
        h1_put(2)

        load_fp4(w4_words, 0)
        load_fp4(w4_words, 1)
        load_planes_side_by_side(fp4_s, w4_scales)
        w3_chunk(1, 0, stage[2])
        w1_chunk(3, 2, 1, across_x_slices(2))
        h1_passes(3, 2)
        gelu(6)
        gelu(7)
        w3_chunk(0, 1, stage[3])
        w3_chunk(1, 1, stage[1])
        read_page(2)
        for s in range(HALF):
            deal(s)
        x_woven = [as_bf16(stage[0], UNIT, UNIT), as_bf16(stage[0], 0, UNIT)]
        weave(nc.scalar.copy, x_dealt[0][:], x_woven[0], 0, S)
        deal(4)
        deal(5)
        h1_put(3)

        late_s = keep.tile([P, 5 * KP], U8, name="late_s", tag="behind_last_scatter", align_bytes=64)
        w3_s = {chunk: late_s[:, KP * n:KP * (n + 1)] for n, chunk in enumerate(w3_order)}
        x_s = [late_s[:, 4 * KP:5 * KP], x_s1[:]]

        def w3_pass(s, a):
            b, t = divmod(s, HALF)
            m = slice(P * t, P * (t + 1))
            nc.tensor.matmul_mx(out=bank[HALF + t][:], lhsT=w3_w[a, b][:, m].bitcast(FP8X4),
                                lhsT_scale=w3_s[a, b][:, m], rhs=x_w[a][:].bitcast(FP8X4), rhs_scale=x_s[a],
                                start=a == 0, stop=a == 1)

        read_page(3)
        deal(6)
        deal(7)
        quantise(x_w[0][:], x_s[0], x_woven[0])
        for s in range(HALF):
            fp4_pass(s, 0, x_w[0][:], x_s[0])
        for chunk in w3_order:
            quantise(w3_w[chunk], w3_s[chunk], w3_woven[chunk])
        for s in range(HALF):
            w3_pass(s, 0)
        weave(nc.scalar.copy, x_dealt[1][:], x_woven[1], 0, SPLIT)
        weave(nc.vector.tensor_copy, x_dealt[1][:], x_woven[1], SPLIT, S)
        quantise(x_w[1][:], x_s[1], x_woven[1])

        def products(s):
            todo = range(1 if s < HALF else 0, 2)
            for a in todo:
                w3_pass(s, a)
            for a in todo:
                fp4_pass(s, a, x_w[a][:], x_s[a])

        def meet(s):
            nc.vector.scalar_tensor_tensor(out=slice_of(x_rows, s), in0=slice_of(x_rows, s),
                                           scalar=own_c[:, s:s + 1], in1=bank[HALF + s % HALF][:],
                                           op0=ALU.mult, op1=ALU.max)

        def finish(s):
            best = slice_of(x_rows, s)
            if s < POOL_SUMS:
                nc.scalar.copy(out=h_buf[s][:], in_=bank[s][:])
                nc.gpsimd.tensor_tensor(out=best, in0=h_buf[s][:], in1=best, op=ALU.add)
            else:
                nc.vector.tensor_tensor(out=best, in0=bank[s % HALF][:], in1=best, op=ALU.add)
            nc.sync.dma_start(out=rows_of(out, s), in_=best)

        products(0)
        meet(0)
        for s in range(last):
            products(s + 1)
            meet(s + 1)
            finish(s)
        finish(last)
